import numpy as np, ml_dtypes
CORES = [2,7,18,23,34]
N = 5
BF = ml_dtypes.bfloat16
V, P, Q, RO, TS = 192, 3, 2, 3, 1024
M, B = 8 * N * V, V // P
def clip(a):
    return np.minimum(np.maximum(np.floor(a), -2 ** 20), 2 ** 20 - 1).astype(np.int64)
def walls(rng, base, size, gap):
    mid = base + size * (rng.random((N, 8, 16, V)) - 0.5)
    h = gap * (16 - np.arange(16)[:, None]) * 0.0625
    l = mid + h * rng.random((N, 8, 16, V)); r = mid - h * rng.random((N, 8, 16, V)); turn = rng.random((N, 8, 1, V)) < 0.25
    return clip(np.where(turn, r, l)), clip(np.where(turn, l, r))
def common(rng):
    return walls(rng, rng.integers(-2 ** 18, 2 ** 18, (N, 8, 1, V)), np.exp2(rng.integers(8, 18, (N, 8, 1, V))), 2.0 ** 17 * rng.random((N, 8, 1, V)))
def slots(rng):
    share = rng.choice(np.array([0.1, 0.4, 0.7, 0.9]), (N, 8, 2, 1, V))
    o = rng.integers(0, M, (N, 8, 16, V)); none = (rng.random((N, 8, 2, 8, V)) < share).reshape(N, 8, 16, V)
    return np.where(none, M, o)
def pack(l, r, o):
    return {"lw": np.ascontiguousarray(l.reshape(N, 128, V)).astype(np.int32), "rw": np.ascontiguousarray(r.reshape(N, 128, V)).astype(np.int32),
            "opts": np.ascontiguousarray(o.reshape(N, 128, V)).astype(np.int32)}
def setup_inputs(rng):
    l, r = common(rng)
    return pack(l, r, slots(rng))
def setup_inputs_ties(rng):
    ix = rng.integers(0, 5, (N, 8, V)); base = 65536 * np.array([0, 0, 12, 12, -13])[:, None] + 2 * rng.integers(-4, 5, (5, 1)); out = []
    for up in (rng.integers(0, 6), 0):
        prof = base + up + rng.integers(0, 2, (5, 16))
        a = prof[ix].transpose(0, 1, 3, 2)
        i = rng.integers(0, 16, (N, 8, 1, V)); d = rng.choice(np.array([-1, 1]), (N, 8, 1, V)) * (rng.random((N, 8, 1, V)) < 0.3)
        far = 65536 * (rng.random((N, 8, 1, V)) < 0.125)
        out.append(a + d * (np.arange(16)[:, None] == i) + far)
    return pack(out[0], out[1], np.where(rng.random((N, 8, 16, V)) < 0.3, M, rng.integers(0, M, (N, 8, 16, V))))
def setup_inputs_bare(rng):
    l, r = common(rng); kinds = np.zeros((7, 16), bool)
    kinds[1, :8] = True; kinds[2, 8:] = True; kinds[3] = True; kinds[4, [0, 15]] = True; kinds[5, [7, 8]] = True; kinds[6, 0] = True
    cls = rng.integers(0, 7, (N, 8, V)); cls[:, 3] = 0; cls[:, 5] = 3
    o = np.where(kinds[cls].transpose(0, 1, 3, 2), rng.integers(0, M, (N, 8, 16, V)), M)
    for g, s, e, d in ((1, 0, -2 ** 20, 1), (6, 15, 2 ** 20 - 1, -1)):
        l[:, g] = e + d * rng.integers(0, 64, (N, 16, V)); r[:, g] = e + d * rng.integers(0, 64, (N, 16, V))
        o[:, g] = M; o[:, g, s] = V * (8 * rng.integers(0, N, (N, V)) + g) + rng.integers(0, B, (N, V))
    return pack(l, r, o)
def setup_inputs_ends(rng):
    l, r = common(rng); o = slots(rng)
    o[:, ::2] = rng.choice(np.array([0, V - 1, V, 8 * V - 1, 8 * V, M - 1, M]), (N, 4, 16, V))
    o[:, 2] = rng.integers(0, M)
    own = V * np.arange(8 * N).reshape(N, 8, 1, 1) + np.arange(V)
    o[:, 1] = np.where(rng.random((N, 16, V)) < 0.5, own[:, 1], o[:, 1])
    o[:, 3, :8] = o[:, 3, :1]; o[:, 3, 8:] = o[:, 3, 8:9]
    here = 8 * V * np.arange(N)[:, None, None]; nxt = 8 * V * ((np.arange(N) + 1) % N)[:, None, None]
    o[:, 5] = nxt + rng.integers(0, 8 * V, (N, 16, V))
    o[:, 7] = np.where(o[:, 7] < M, here + rng.integers(0, 8 * V, (N, 16, V)), M)
    return pack(l, r, o)
def setup_inputs_late(rng):
    bump = rng.random((N, 8, 1, V)) < 0.0625; bump[:, 4] = False
    l = rng.integers(-2 ** 12, 2 ** 12, (16, 1)) + bump
    r = l + rng.choice(np.array([-3, 0, 3, 5001]), (16, 1))
    z = rng.integers(0, 8, (N, 8, 2, 1, V)); s = np.arange(8)[:, None]
    has = np.where(rng.random((N, 8, 2, 1, V)) < 0.4, s == z, s >= z).reshape(N, 8, 16, V)
    o = np.where(has, rng.integers(0, M, (N, 8, 16, V)), M)
    o[:, 4] = V * (8 * rng.integers(0, N, (N, 16, V)) + 4) + rng.integers(0, V, (N, 16, V))
    return pack(l, r, o)
def setup_inputs_spread(rng):
    base = rng.choice(np.array([-1.0, 1.0]), (N, 8, 1, V)) * np.exp2(20 * rng.random((N, 8, 1, V)))
    l, r = walls(rng, base, np.abs(base) * rng.random((N, 8, 1, V)), np.exp2(18 * rng.random((N, 8, 1, V))))
    e = rng.integers(1, 5, (1, 8, 1, 1))
    o = np.minimum((M * rng.random((N, 8, 16, V)) ** e).astype(np.int64), M - 1)
    share = rng.random((N, 8, 1, V)); share[rng.integers(0, N)] = 0.0
    return pack(l, r, np.where(rng.random((N, 8, 16, V)) < share, M, o))
def check_inputs(d):
    bad = []
    for k, lo, hi in (("lw", -2 ** 20, 2 ** 20 - 1), ("rw", -2 ** 20, 2 ** 20 - 1), ("opts", 0, M)):
        if np.min(d[k]) < lo or np.max(d[k]) > hi: bad.append("range of " + k)
    return bad
def world(a, last):
    w = a.reshape(N, 8, 16, V).transpose(2, 0, 1, 3).reshape(16, M).astype(np.int32)
    return np.concatenate([w, np.full((16, 1), last, np.int32)], axis=1)
def back(w):
    return np.ascontiguousarray(w[:, :M].reshape(16, N, 8, V).transpose(1, 2, 0, 3)).reshape(N, 128, V).astype(np.float32)
def inner(L, R, ix):
    return np.concatenate([R[:, ix[:8]], -L[:, ix[8:]]], axis=1)
def reference(lw, rw, opts):
    L, R, O = world(lw, 0), world(rw, 0), world(opts, M)
    temp = (TS * np.arange(16, dtype=np.int32))[:, None]; s16 = np.arange(16); left = (s16 < 8)[:, None]
    for t in range(RO):
        nL, nR, nO = L.copy(), R.copy(), O.copy()
        v = np.tile(B * (t % P) + np.arange(B), 8 * N); c = V * np.repeat(np.arange(8 * N), B) + v
        o = O[:, c]; xl, xr = L[:, c], R[:, c]; has = o < M
        u = inner(L, R, o); gone = np.zeros(o.shape, bool)
        for q in range(Q):
            p = s16 ^ (1 + (t + 3 * q) % 7); up = u[:, p]
            ge = np.all(up >= u, axis=0); eq = np.all(up == u, axis=0)
            gone = gone | (has & has[p] & ge & (~eq | (p < s16)[:, None]))
        sl = (v + t) & 7; k = O[np.where(left, 8 + sl, sl), o]
        kl, kr = L[:, k], R[:, k]; yl, yr = xl[:, None, :], xr[:, None, :]
        under = np.all((kl[:, :8] <= yl) & (kr[:, :8] <= yr), axis=0); over = np.all((kl[:, 8:] >= yl) & (kr[:, 8:] >= yr), axis=0)
        rev = (has & ~gone & (k < M) & np.concatenate([under, over], axis=0)).reshape(2, 8, -1).astype(np.int64)
        first = (rev == 1) & (np.add.accumulate(rev, axis=1) == 1)
        ch = np.where(np.any(first, axis=1), np.add.reduce(first * k.reshape(2, 8, -1), axis=1), M)
        ent = O[s16[:, None], np.repeat(ch, 8, axis=0)]
        n = np.where(has & ~gone & ~first.reshape(16, -1), o, ent); hn = n < M
        w = np.where(hn[None], inner(L, R, n), -2 ** 23)
        l = np.where(np.any(hn[:8], axis=0)[None], np.max(w[:, :8], axis=1) - temp, xl)
        r = np.where(np.any(hn[8:], axis=0)[None], temp - np.max(w[:, 8:], axis=1), xr)
        low = l < r; mid = (l + r) >> 1
        nL[:, c] = np.where(low, mid, l); nR[:, c] = np.where(low, mid, r); nO[:, c] = n
        L, R, O = nL, nR, nO
    return {"yl": back(L), "yr": back(R), "yo": back(O)}

@@ -1,0 +1,603 @@
+import numpy as np
+from concourse.bass import DstId, RemoteDMATransfer
+from concourse.mybir import dt, AluOpType, AxisListType, ActivationFunctionType
+
+A_ = AluOpType
+COPY = ActivationFunctionType.Copy
+IDENT = ActivationFunctionType.Identity
+RELU = ActivationFunctionType.Relu
+G1, R1, B1 = 2880, 576, 192
+WC = 8 * G1
+EC = 43264
+BIG = 8388608.0
+OFF = 6291456.0
+PN = [576, 192, 192]
+
+
+def _f(n): return ("sbuf", [128, n], "float32")
+def _i(n): return ("sbuf", [128, n], "int32")
+def _b(n): return ("sbuf", [128, n], "bfloat16")
+def _u(n): return ("sbuf", [128, n], "uint16")
+
+
+SCRATCH = {
+    "W": _f(WC + B1), "LI": _i(192), "RI": _i(192), "OI": _i(192),
+    "SB0": _f(576), "SB1": _f(192), "SB2": _f(192), "SB3": _f(192), "NB0": _f(576), "NB1": _f(192), "NB2": _f(192),
+    "i1": _i(192), "i2": _i(192), "i3": _i(192), "f1": _f(192), "f2": _f(192), "f3": _f(192), "f4": _f(192), "CD": _f(192),
+    "PI": _i(1), "pc": _i(16), "fc": _f(40), "CI": _f(176), "REL": _f(176), "tmp": _f(176), "tmp2": _f(176),
+    "QF": _f(512), "QB": _b(512), "GF": _f(512), "EM": _b(176), "AD": _b(1120), "BM": _b(176), "C1": _b(144),
+    "LT": _b(128), "ID": _b(128), "IDF": _f(512), "UPC": _b(192),
+    "j1": _i(32), "j2": _i(32), "j3": _i(32), "j4": _i(8), "j5": _i(8), "j6": _i(8), "j7": _i(8), "j8": _i(8),
+    "SEL": _u(16), "XBL": _u(32), "CDL": _u(12), "DSL": _u(8), "LU": _u(192), "LO": _u(192), "NO": _f(192),
+    "XR": _f(1536), "XN": _f(1536), "XW": _f(384), "RS": _f(1024),
+    "U": _f(1024), "T0": _f(1024), "T1": _f(1024), "TL": _f(1024), "D1": _f(512), "D2": _f(512),
+    "IA1": _b(512), "IB1": _b(512), "IA2": _b(512), "IB2": _b(512), "VR": _b(1024), "VL": _b(1024),
+    "K": _f(64), "kz": _f(64), "ky": _f(64), "kf": _f(64), "KH": _b(64), "KL": _b(64), "LKR": _u(64), "LKL": _u(64),
+    "m1": _f(64), "m2": _f(64), "GX": _b(64), "FI": _b(64), "REV": _b(64), "FH": _b(64), "FL": _b(64),
+    "DP": _f(128), "DS": _f(128), "EN": _f(128), "cz": _f(8), "cy": _f(8), "CLS": _u(8),
+    "o1": _f(64), "o2": _f(64), "o3": _f(64), "n1": _f(64), "nz": _f(64), "ny": _f(64), "LN": _u(64),
+    "U2": _f(1024), "SC": _f(1024), "we": _f(128), "wh": _f(128), "ww": _f(128), "wn": _f(128), "ws": _f(64), "wl": _f(64),
+    "wi": _i(64), "wj": _i(64), "YL": _f(64), "YO": _f(64), "yy": _f(192), "y4": _f(64),
+    "PZ1": ("psum", [128, 512], "float32"), "PZ2": ("psum", [128, 512], "float32"), "PCN": ("psum", [128, 512], "float32"),
+    "PPF": ("psum", [128, 512], "float32"), "PDM": ("psum", [128, 512], "float32"), "PCH": ("psum", [128, 512], "float32"),
+    "PP2": ("psum", [128, 512], "float32"), "PG2": ("psum", [128, 512], "float32"),
+    "DA0": ("dram", [256, 576], "float32"), "DA1": ("dram", [256, 192], "float32"), "DA2": ("dram", [256, 192], "float32"),
+}
+SEMAPHORES = ["qv", "qs", "qp", "qg", "ls", "ldO", "ldL", "ldR", "go1", "go2"] + [
+    "%s%d" % (k, e) for k in ("arr", "own", "nbd", "fA", "fB", "dA", "oO", "oR", "oL") for e in range(3)]
+
+
+def pl(bits):
+    return sum(1 << b for b in bits)
+
+
+def dst(topo, c):
+    rid, pid, _ = topo.addr(c)
+    return DstId(rid=rid, pnc=pid)
+
+
+def plan(T, topo):
+    cores = list(T.cores)
+    role, of = {}, {}
+    for r, c in enumerate(cores):
+        near = [h for h in topo.cores_of(c) if topo.die(h) == topo.die(c) and h not in cores]
+        far = [h for h in topo.cores_of(c) if topo.die(h) != topo.die(c) and h not in cores]
+        off = [q for q, d in enumerate(cores) if topo.chip(d) != topo.chip(c)]
+        for q, h in zip(off, near + far):
+            role[h] = {"rank": r, "A": q, "feed": cores[q], "fwd": []}
+            of[(r, q)] = h
+    for (r, q), h in of.items():
+        if topo.die(cores[r]) != topo.die(cores[q]):
+            for r2 in range(len(cores)):
+                if r2 != r and topo.chip(cores[r2]) == topo.chip(cores[r]) and topo.die(cores[r2]) == topo.die(cores[q]):
+                    role[h]["feed"] = of[(r2, q)]
+                    role[of[(r2, q)]]["fwd"].append(h)
+    return cores, role
+
+
+def calls_of(info, cores):
+    if info["feed"] in cores:
+        return [[0], [1, 2, 3, 4], [5, 6], [7]]
+    return [[0, 1, 2, 3, 4, 5, 6, 7]]
+
+
+def helper(g, core, T, topo, cores, role):
+    info = role[core]
+    rc = cores[info["rank"]]
+    eng = topo.engines(core, rc)
+    direct = info["feed"] in cores
+    ls = 0
+    for e in range(3):
+        n, buf, fa = PN[e], T["DA%d" % e], T.sem["fA%d" % e]
+        got = len(topo.engines(info["feed"], core)) * (1 if direct else 2)
+        g.wait_ge(fa, got)
+        if direct:
+            g.sync.wait_ge(fa, got)
+            g.sync.dma_start(buf[128:240, :], buf[0:112, :]).then_inc(T.sem["dA%d" % e], 16)
+        for h in info["fwd"]:
+            en = topo.engines(core, h)
+            g.remote_dma_fused([RemoteDMATransfer(dst_ids=[dst(topo, h)] * 2, dma_engine_mask=pl(en), remote_sem=fa,
+                                                  srcs=[buf[0:128, :]], dsts=[buf[0:128, :], buf[128:256, :]])], local_sem=T.sem.ls)
+            ls += len(en)
+        if e:
+            g.wait_ge(T.sem["go%d" % e], 1)
+        for ci, call in enumerate(calls_of(info, cores)):
+            if ci == 1:
+                g.wait_ge(T.sem["dA%d" % e], 16)
+            w = len(eng) // len(call)
+            trs = []
+            for j, k in enumerate(call):
+                c0 = k * G1 + info["A"] * R1 + (e - 1) * B1 * (e > 0)
+                trs.append(RemoteDMATransfer(dst_ids=[dst(topo, rc)], dma_engine_mask=pl(eng[j * w:(j + 1) * w]), remote_sem=T.sem["arr%d" % e],
+                                             srcs=[buf[16 * k:16 * k + 128, :]], dsts=[T.W[:, c0:c0 + n]]))
+                ls += w
+            g.remote_dma_fused(trs, local_sem=T.sem.ls)
+    g.wait_ge(T.sem.ls, ls)
+
+
+def rank_program(g, core, T, topo):
+    cores, role = plan(T, topo)
+    rank = T.rank_of(core)
+    if rank is None:
+        if core in role:
+            helper(g, core, T, topo, cores, role)
+        return
+    mine = [h for h in role if role[h]["rank"] == rank]
+    near = [q for q, c in enumerate(cores) if q != rank and topo.chip(c) == topo.chip(core)]
+    arr_n = sum(16 * len(calls_of(role[h], cores)) for h in mine)
+    V, S, PE, Y = g.vector, g.scalar, g.tensor, g.sync
+    Q = {"v": V, "s": S, "p": PE, "g": g, "y": Y}
+    QS = {"v": "qv", "s": "qs", "p": "qp", "g": "qg"}
+    cnt, known, lastw, readers, lastx = {}, {q: {} for q in Q}, {}, {}, {}
+
+    def need(q, tok):
+        _, sem, c, clock = tok
+        if known[q].get(sem, 0) >= c:
+            return
+        Q[q].wait_ge(T.sem[sem], c)
+        for s2, c2 in clock.items():
+            known[q][s2] = max(known[q].get(s2, 0), c2)
+        known[q][sem] = max(known[q].get(sem, 0), c)
+
+    def deps(q, rd, wr, ps):
+        toks = []
+        for k in rd:
+            if k in lastw:
+                toks.append(lastw[k])
+        for k in wr:
+            if k in lastw:
+                toks.append(lastw[k])
+            toks += readers.get(k, [])
+        for k in ps:
+            if k in lastx:
+                toks += [t for t in lastx[k].values() if t[0] != q]
+        best = {}
+        for t in toks:
+            if q == "p" and t[0] == "p":
+                continue
+            if t[1] not in best or best[t[1]][2] < t[2]:
+                best[t[1]] = t
+        for t in sorted(best.values(), key=lambda t: -t[2]):
+            need(q, t)
+
+    def note(q, rd, wr, ps, tok):
+        for k in rd:
+            readers.setdefault(k, [])
+            readers[k] = [t for t in readers[k] if not (t[0] == q and t[1] == tok[1])] + [tok]
+        for k in wr:
+            lastw[k] = tok
+            readers[k] = []
+        for k in ps:
+            lastx.setdefault(k, {})
+            lastx[k][q] = tok
+
+    def op(q, fn, rd=(), wr=(), ps=()):
+        deps(q, rd, wr, ps)
+        sem = QS[q]
+        c = cnt.get(sem, 0) + 1
+        cnt[sem] = c
+        fn(Q[q]).then_inc(T.sem[sem], 1)
+        clock = dict(known[q])
+        clock[sem] = c
+        note(q, rd, wr, ps, (q, sem, c, clock))
+
+    def dma(q, sem, pairs, rd=(), wr=()):
+        deps(q, rd, wr, ())
+        for o, i in pairs:
+            Q[q].dma_start(o, i).then_inc(T.sem[sem], 16)
+        cnt[sem] = cnt.get(sem, 0) + 16 * len(pairs)
+        clock = dict(known[q])
+        clock[sem] = cnt[sem]
+        note(q, rd, wr, (), (q, sem, cnt[sem], clock))
+
+    def split(xs):
+        ks = [x[0] for x in xs if isinstance(x, tuple)]
+        return [k for k in ks if k[0] != "P" or k == "PI"], [k for k in ks if k[0] == "P" and k != "PI"]
+
+    def raw(x):
+        return x[1] if isinstance(x, tuple) else x
+
+    def emit(q, fn, ins, out):
+        r, rp = split(ins)
+        w, wp = split([out])
+        return op(q, fn, r, w, rp + wp)
+
+    def ts(out, a, s1, o1, s2=None, o2=None):
+        if o2 is None:
+            return emit("v", lambda e: e.tensor_scalar(raw(out), raw(a), raw(s1), None, o1), [a, s1], out)
+        return emit("v", lambda e: e.tensor_scalar(raw(out), raw(a), raw(s1), raw(s2), o1, o2), [a, s1, s2], out)
+
+    def tt(out, a, b, o, more=()):
+        return emit("v", lambda e: e.tensor_tensor(raw(out), raw(a), raw(b), o), [a, b] + list(more), out)
+
+    def cp(out, a, more=()):
+        return emit("v", lambda e: e.tensor_copy(raw(out), raw(a)), [a] + list(more), out)
+
+    def act(out, a, f=COPY, scale=1.0, more=(), bias=0.0):
+        return emit("s", lambda e: e.activation(raw(out), raw(a), f, bias=raw(bias), scale=scale), [a, bias] + list(more), out)
+
+    def mm(out, l, r, start, stop):
+        return emit("p", lambda e: e.matmul(raw(out), raw(l), raw(r), start, stop), [l, r], out)
+
+    def C(name, a, b=None, st=None):
+        return (name, T[name][:, a:b:st])
+
+    def X(name):
+        return (name, T[name][:])
+
+    dma("y", "ldO", [(T.OI[:], T.opts[:])], wr=["OI"])
+    dma("y", "ldR", [(T.RI[:], T.rw[:])], wr=["RI"])
+    dma("y", "ldL", [(T.LI[:], T.lw[:])], wr=["LI"])
+    op("g", lambda e: e.iota(T.PI[:], [[0, 1]], 0, 1), wr=["PI"])
+    op("g", lambda e: e.iota(T.j1[:], [[1, 32]], 0, 0), wr=["j1"])
+    op("g", lambda e: e.iota(T.CI[:], [[1, 176]], 0, 0, allow_small_or_imprecise_dtypes=True), wr=["CI"])
+    npc, nfc, nls = [0], [0], [0]
+
+    def icol(shop, val):
+        k = npc[0]
+        npc[0] += 1
+        o = ("pc%d" % k, T.pc[:, k:k + 1])
+        ts(o, X("PI"), val, shop)
+        return o
+
+    def newf():
+        k = nfc[0]
+        nfc[0] += 1
+        return ("fc%d" % k, T.fc[:, k:k + 1])
+
+    def fcol(a, s1, o1):
+        o = newf()
+        ts(o, a, s1, o1)
+        return o
+
+    hh = icol(A_.logical_shift_right, 4)
+    p3i = icol(A_.bitwise_and, 8)
+    p4i = icol(A_.bitwise_and, 16)
+    p15 = icol(A_.bitwise_and, 15)
+    p7 = icol(A_.bitwise_and, 7)
+    pg = icol(A_.bitwise_and, 96)
+    p120 = icol(A_.bitwise_and, 120)
+    ub = {1: icol(A_.bitwise_and, 1), 2: icol(A_.bitwise_and, 2), 4: icol(A_.bitwise_and, 4)}
+    H = fcol(hh, float(G1), A_.mult)
+    nH = fcol(hh, -float(G1), A_.mult)
+    n = X("OI")
+    ts(X("i1"), n, 1.0 / 192, A_.mult, -95.5 / 192, A_.add)
+    ts(X("i2"), n, 1.0 / 1536, A_.mult, -767.5 / 1536, A_.add)
+    ts(X("i3"), n, 1.0 / 64, A_.mult, -31.5 / 64, A_.add)
+    ts(X("f4"), n, 7680, A_.is_ge, EC - 2880.0, A_.mult)
+    ts(X("f1"), X("i1"), 2304, A_.mult)
+    ts(X("f2"), X("i2"), -22464, A_.mult)
+    ts(X("f3"), X("i3"), 128, A_.mult)
+    tt(X("f4"), X("f4"), n, A_.add)
+    tt(X("f1"), X("f1"), X("f2"), A_.add)
+    tt(X("f3"), X("f3"), X("f4"), A_.add)
+    for t in range(3):
+        b, w = t * B1, 64 * t
+        tt(C("SB0", b + 128, b + 192), C("f1", w, w + 64), C("f3", w, w + 64), A_.add)
+        cp(C("SB0", b, b + 64), C("RI", w, w + 64))
+        ts(C("SB0", b + 64, b + 128), C("LI", w, w + 64), -1.0, A_.mult)
+
+    def send(e, name):
+        deps("g", [name], [], ())
+        offs = [h for h in role if role[h]["feed"] == core]
+        en = topo.engines(core, offs[0])
+        trs = [RemoteDMATransfer(dst_ids=[dst(topo, h) for h in offs], dma_engine_mask=pl(en), remote_sem=T.sem["fA%d" % e],
+                                 srcs=[T[name][:]], dsts=[T["DA%d" % e][0:128, :] for h in offs])]
+        nls[0] += len(en)
+        for q in near:
+            e2 = [x for x in topo.engines(core, cores[q]) if x not in en]
+            trs.append(RemoteDMATransfer(dst_ids=[dst(topo, cores[q])], dma_engine_mask=pl(e2), remote_sem=T.sem["fB%d" % e],
+                                         srcs=[T[name][:]], dsts=[T["NB%d" % e][:]]))
+            nls[0] += len(e2)
+        g.remote_dma_fused(trs, local_sem=T.sem.ls)
+
+    def put(e, sem, name, src, rd):
+        nn = PN[e]
+        c0 = src * R1 + (e - 1) * B1 * (e > 0)
+        pairs = [(T.W[:, c0:c0 + nn], T[name][:])]
+        for k in range(1, 8):
+            c = c0 + k * G1
+            pairs.append((T.W[0:128 - 16 * k, c:c + nn], T[name][16 * k:128, :]))
+            pairs.append((T.W[128 - 16 * k:128, c:c + nn], T[name][0:16 * k, :]))
+        dma("y", sem + str(e), pairs, rd=rd, wr=[sem])
+
+    def spread(e, name):
+        deps("y", [], ["W"], ())
+        put(e, "own", name, rank, [name])
+        for q in near:
+            h = [h for h in role if role[h]["feed"] == cores[q]][0]
+            Y.wait_ge(T.sem["fB%d" % e], len([x for x in topo.engines(cores[q], core) if x not in topo.engines(cores[q], h)]))
+            put(e, "nbd", "NB%d" % e, q, [])
+
+    send(0, "SB0")
+    spread(0, "SB0")
+    op("g", lambda e: e.iota(T.RS[:], [[0, 1024]], 0, 0, allow_small_or_imprecise_dtypes=True), wr=["RS"])
+    op("g", lambda e: e.affine_select(T.RS[:], T.RS[:], [[0, 128], [1, 8]], A_.not_equal, -2.0 ** 25, 0, 0), rd=["RS"], wr=["RS"])
+    nH64 = fcol(nH, 64.0, A_.add)
+    nH128 = fcol(nH, 128.0, A_.add)
+    p15f = fcol(p15, 1.0, A_.mult)
+    p3f = fcol(p3i, 1.0, A_.mult)
+    pf = fcol(X("PI"), 1.0, A_.mult)
+    j5 = X("j5")
+    ts(j5, C("j1", 0, 8), 16, A_.mult, p15f, A_.add)
+    ts(X("j6"), j5, 5, A_.logical_shift_right)
+    ts(X("j7"), j5, 24, A_.bitwise_and)
+    ts(X("j8"), j5, 7, A_.bitwise_and)
+    ts(X("j6"), X("j6"), 192, A_.mult, 128, A_.add)
+    ts(X("j7"), X("j7"), 2, A_.mult)
+    tt(X("j8"), X("j8"), X("j6"), A_.add)
+    tt(X("j8"), X("j8"), X("j7"), A_.add)
+    cp(C("CDL", 0, 6), C("j8", 0, 6))
+    ts(C("CDL", 6, 12), C("j8", 0, 6), 8, A_.add)
+    act(X("CD"), ("SB0", T.SB0[:].indirect(T.CDL[:])), more=[("CDL", 0)])
+    ts(X("j2"), X("j1"), 24, A_.bitwise_and)
+    ts(X("j3"), X("j1"), 7, A_.bitwise_and)
+    ts(X("j2"), X("j2"), 2, A_.mult, p3f, A_.add)
+    tt(X("j2"), X("j2"), X("j3"), A_.add)
+    cp(X("XBL"), X("j2"))
+    temp = fcol(p15, 1024.0, A_.mult)
+    tempo = fcol(temp, -OFF, A_.add)
+    ntemp = fcol(temp, -1.0, A_.mult)
+
+    def own_walls(t):
+        b = t * B1
+        act(C("XR", 512 * t, 512 * t + 512), ("SB0", T.SB0[:, b:b + 64].indirect(T.XBL[:])), more=[("XBL", 0)])
+        act(C("XN", 512 * t, 512 * t + 512), ("SB0", T.SB0[:, b + 64:b + 128].indirect(T.XBL[:])), more=[("XBL", 0)])
+        act(C("XW", 128 * t, 128 * t + 128, 2), C("SB0", b + 64, b + 128), IDENT, scale=-1.0, bias=tempo)
+        act(C("XW", 128 * t + 1, 128 * t + 128, 2), C("SB0", b, b + 64), IDENT, scale=-1.0, bias=tempo)
+
+    def sel2(base, col, big, full):
+        x, y0, y1, y2 = newf(), newf(), newf(), newf()
+        ts(x, col, big, A_.mult)
+        tt(y0, base, x, A_.add)
+        tt(y1, base, x, A_.subtract)
+        ts(y2, y1, full, A_.add)
+        return y0, y2
+
+    A3 = sel2(pf, p3i, 125.0, 1000.0)
+    for a in range(2):
+        for b in range(2):
+            o = 128 * (2 * a + b)
+            ts(C("QF", o, o + 128), C("CI", 0, 128), -8.0 * (b - a), A_.add, A3[a], A_.is_equal)
+    act(X("QB"), X("QF"))
+    gb = fcol(p3i, 2.0, A_.mult)
+    gc, gd = newf(), newf()
+    tt(gc, gb, pg, A_.add)
+    tt(gd, gc, p7, A_.add)
+    A4 = sel2(gd, p4i, 100.0, 1600.0)
+    for b in range(2):
+        for a in range(2):
+            o = 128 * (2 * b + a)
+            ts(C("GF", o, o + 128), C("CI", 0, 128), -8.0 * a, A_.add, A4[b], A_.is_equal)
+    for bank, M in (("PP2", "QF"), ("PG2", "GF")):
+        for x in range(2):
+            for a in range(2):
+                o = 128 * (2 * x + a)
+                mm(C(bank, 96 * x, 96 * x + 96), C(M, o, o + 128), C("CD", 96 * a, 96 * a + 96), a == 0, a == 1)
+    op("v", lambda e: e.memset(T.W[:, WC:WC + 128], -BIG), wr=["Wemp"])
+    op("v", lambda e: e.memset(T.W[:, WC + 128:WC + 192], float(EC)), wr=["Wemp"])
+    ts(X("f1"), C("PP2", 0, 192), H, A_.is_lt, float(WC), A_.mult)
+    tt(X("f2"), X("f1"), C("PP2", 0, 192), A_.add)
+    ts(X("f3"), C("PG2", 0, 192), H, A_.is_lt, float(WC), A_.mult)
+    tt(X("f4"), X("f3"), C("PG2", 0, 192), A_.add)
+
+    def lists(t):
+        for side in range(2):
+            i, o = 96 * side + 32 * t, 64 * t + 32 * side
+            ts(C("LU", o, o + 32), C("f2", i, i + 32), nH64 if side else nH, A_.add, float(WC + 64 * side), A_.min)
+        for b in range(2):
+            ts(C("LO", 64 * t + b, 64 * t + 64, 2), C("f4", 96 * b + 32 * t, 96 * b + 32 * t + 32), nH128, A_.add, float(WC + 128), A_.min)
+
+    def empties(t):
+        for side in range(2):
+            i, o = 96 * side + 32 * t, 64 * t + 32 * side
+            ts(C("NO", o, o + 32), C("f2", i, i + 32), EC - 32.0, A_.is_ge)
+
+    lists(0)
+    h16 = fcol(hh, 16.0, A_.mult)
+    ts(X("REL"), X("CI"), h16, A_.subtract)
+    ts(X("EM"), X("REL"), 24.0, A_.is_equal)
+    act(X("BM"), X("EM"), scale=-2.0 ** 30)
+
+    def diffs(ds, hbs):
+        for d in ds:
+            tt(C("AD", 160 * d, 160 * d + 160), C("EM", 8, 168), C("EM", 8 - d, 168 - d), A_.subtract)
+        for hb in hbs:
+            u = fcol(ub[hb], 0.5 / hb, A_.mult)
+            ts(C("UPC", 64 * (hb // 2), 64 * (hb // 2) + 64), C("CI", 0, 64), 0.0, A_.mult, u, A_.add)
+
+    ts(X("ID"), C("CI", 0, 128), pf, A_.is_equal)
+    diffs((1, 4), (1, 4))
+    ts(X("j6"), j5, 31, A_.bitwise_and)
+    ts(X("j7"), j5, 5, A_.logical_shift_right)
+    ts(X("j6"), X("j6"), 32, A_.mult, 8, A_.add)
+    ts(X("j7"), X("j7"), 8, A_.mult)
+    tt(X("j6"), X("j6"), X("j7"), A_.add)
+
+    def sels(t):
+        ts(X("j4"), j5, t, A_.add)
+        ts(X("j4"), X("j4"), 7, A_.bitwise_and)
+        tt(X("j4"), X("j4"), X("j6"), A_.add)
+        cp(C("SEL", 4 * t, 4 * t + 4), C("j4", 0, 4))
+
+    sels(0)
+    own_walls(0)
+    act(X("PP2"), C("XN", 0, 512))
+    empties(0)
+    p8f = fcol(p120, 1.0, A_.mult)
+    ts(X("tmp"), X("CI"), p8f, A_.subtract)
+    ts(X("C1"), C("tmp", 0, 144), 8.0, A_.is_equal)
+    ts(C("tmp2", 0, 128), C("tmp", 0, 128), 8.0, A_.is_lt)
+    ts(C("tmp", 0, 128), C("CI", 0, 128), pf, A_.is_gt)
+    tt(C("tmp2", 0, 128), C("tmp2", 0, 128), C("tmp", 0, 128), A_.mult)
+    ts(C("tmp", 0, 128), C("CI", 0, 128), pf, A_.is_equal, -0.5, A_.mult)
+    tt(X("LT"), C("tmp2", 0, 128), C("tmp", 0, 128), A_.add)
+    HmE = fcol(H, -float(EC), A_.add)
+    EH = fcol(nH, EC + 128.0, A_.add)
+    s64 = fcol(p3i, 8.0, A_.mult)
+    capN = fcol(s64, float(WC), A_.add)
+    nHs = newf()
+    tt(nHs, s64, nH, A_.add)
+    p34 = fcol(p3i, 4.0, A_.mult)
+    p347 = newf()
+    tt(p347, p34, p7, A_.add)
+    ts(C("j2", 0, 8), C("j1", 0, 8), 4, A_.bitwise_and)
+    ts(C("j3", 0, 8), C("j1", 0, 8), 3, A_.bitwise_and)
+    ts(C("j2", 0, 8), C("j2", 0, 8), 16, A_.mult, p347, A_.add)
+    ts(C("j3", 0, 8), C("j3", 0, 8), 8, A_.mult)
+    tt(C("j2", 0, 8), C("j2", 0, 8), C("j3", 0, 8), A_.add)
+    cp(X("DSL"), C("j2", 0, 8))
+
+    def win(L, lo, hi):
+        return ("W", T.W[:].indirect(T[L][:, lo:hi]))
+
+    def wm(L):
+        return [(L, 0), ("own", 0), ("nbd", 0), ("Wemp", 0)]
+
+    for t in range(3):
+        xb = 512 * t
+        for q in "vs":
+            Q[q].wait_ge(T.sem["arr%d" % t], arr_n)
+        cp(("Ua", T.U[:, 0:512]), win("LU", 64 * t, 64 * t + 32), more=wm("LU"))
+        act(("Ub", T.U[:, 512:1024]), win("LU", 64 * t + 32, 64 * t + 64), more=wm("LU"))
+        act(X("T0"), win("LO", 64 * t, 64 * t + 64), more=wm("LO"))
+        for z, k in enumerate((1 + t % 7, 1 + (t + 3) % 7)):
+            D, IA, IB, PZ = "D%d" % (z + 1), "IA%d" % (z + 1), "IB%d" % (z + 1), "PZ%d" % (z + 1)
+            hb = 4 if k >= 4 else 2 if k >= 2 else 1
+            m = 4 // hb
+            off, where = 0, {}
+            for r in range(2 * hb):
+                if r & hb:
+                    continue
+                tt((D, T[D][:, off:off + 128 * m]), ("Ua", T.U[:, r ^ k::2 * hb]), ("Ub", T.U[:, r::2 * hb]), A_.subtract)
+                for i in range(m):
+                    where[r + 2 * hb * i] = off + i
+                off += 128 * m
+            act(X(IA), X(D), RELU)
+            act(X(IB), X(D), RELU, scale=-1.0)
+            o = C(PZ, 0, 64)
+            mm(o, X("ID"), C("UPC", 64 * (hb // 2), 64 * (hb // 2) + 64), True, False)
+            todo = [(a, s, x) for x in (0, 1) for a in range(2) for s in sorted(where)]
+            for i, (a, s, x) in enumerate(todo):
+                qs, lo, d = 8 * a + s, where[s] + a * m, (s ^ k) - s
+                l = C("BM", 24 - qs, 152 - qs) if x else C("AD", 160 * d + 16 - qs, 160 * d + 144 - qs)
+                mm(o, l, C(IB if x else IA, lo, lo + 2 * m * 63 + 1, 2 * m), False, i == len(todo) - 1)
+        emit("v", lambda e: e.transpose(T.T1[:], T.T0[:]), [("T0", 0)], ("T1", 0))
+        cp(X("K"), ("T1", T.T1[:].indirect(T.SEL[:, 4 * t:4 * t + 4])), more=[("SEL", 0)])
+        ts(X("kz"), X("K"), H, A_.is_lt, float(WC), A_.mult)
+        tt(X("ky"), X("kz"), X("K"), A_.add)
+        ts(X("LKL"), X("ky"), nH64, A_.add, float(WC + 64), A_.min)
+        ts(X("LKR"), X("ky"), nH, A_.add, float(WC), A_.min)
+        for side in range(2):
+            act(("TL%d" % side, T.TL[:, 512 * side:512 * side + 512]), win("LKL", 32 * side, 32 * side + 32), more=wm("LKL"))
+            tt(C("VR", 512 * side, 512 * side + 512), win("LKR", 32 * side, 32 * side + 32), C("XR", xb, xb + 512), (A_.is_gt, A_.is_lt)[side], more=wm("LKR"))
+        act(X("kf"), X("K"), IDENT, bias=-float(EC))
+        act(X("KH"), X("kf"))
+        tt(X("m1"), C("PZ1", 0, 64), C("NO", 64 * t, 64 * t + 64), A_.max)
+        tt(X("m2"), C("PZ2", 0, 64), X("m1"), A_.max)
+        ts(X("GX"), X("m2"), 0.25, A_.is_gt)
+        for side in range(2):
+            tt(C("VL", 512 * side, 512 * side + 512), ("TL%d" % side, T.TL[:, 512 * side:512 * side + 512]), X("PP2"), (A_.is_lt, A_.is_gt)[side])
+        tt(X("KL"), X("kf"), X("KH"), A_.subtract)
+        o = C("PCN", 0, 64)
+        for i in range(16):
+            mm(o, C("EM", 24 - i, 152 - i), C("VR", i, None, 16), i == 0, False)
+        mm(o, X("ID"), X("GX"), False, False)
+        for i in range(16):
+            mm(o, C("EM", 24 - i, 152 - i), C("VL", i, None, 16), False, i == 15)
+        ts(X("REV"), o, 0.0, A_.is_equal)
+        mm(C("PPF", 0, 64), X("LT"), X("REV"), True, True)
+        ts(X("FI"), C("PPF", 0, 64), 0.0, A_.is_lt)
+        tt(X("FH"), X("FI"), X("KH"), A_.mult)
+        tt(X("FL"), X("FI"), X("KL"), A_.mult)
+        for side in range(2):
+            for a in range(2):
+                oo = C("PDM", 64 * side + 32 * a, 64 * side + 32 * a + 32)
+                l = C("QB", 128 * (2 * a + side), 128 * (2 * a + side) + 128)
+                mm(oo, l, C("GX", 32 * side, 32 * side + 32), True, False)
+                mm(oo, l, C("FI", 32 * side, 32 * side + 32), False, True)
+        o = C("PCH", 0, 8)
+        for x in ("FH", "FL"):
+            for c in range(8):
+                mm(o, C("C1", 8 - c, 136 - c), C(x, c, None, 8), x == "FH" and c == 0, x == "FL" and c == 7)
+        oc = C("SB0", t * B1 + 128, t * B1 + 192)
+        act(X("DP"), C("PDM", 0, 128))
+        act(X("DS"), ("DP", T.DP[:].indirect(T.DSL[:])), more=[("DSL", 0)])
+        tt(X("o1"), C("DS", 0, 64), C("DS", 64, 128), A_.add)
+        tt(X("o2"), X("o1"), oc, A_.mult)
+        ts(X("cz"), o, HmE, A_.is_lt, float(WC), A_.mult)
+        tt(X("cy"), X("cz"), o, A_.add)
+        ts(X("CLS"), X("cy"), EH, A_.add, float(WC + 128), A_.min)
+        tt(X("o3"), oc, X("o2"), A_.subtract)
+        tt(X("EN"), win("CLS", 0, 8), X("DS"), A_.mult, more=wm("CLS"))
+        tt(X("n1"), C("EN", 0, 64), C("EN", 64, 128), A_.add)
+        sb = "SB%d" % (t + 1)
+        nw = C(sb, 128, 192)
+        tt(nw, X("n1"), X("o3"), A_.add)
+        ts(X("nz"), nw, H, A_.is_lt, float(WC), A_.mult)
+        tt(X("ny"), X("nz"), nw, A_.add)
+        ts(X("LN"), X("ny"), nHs, A_.add, capN, A_.min)
+        cp(("U2a", T.U2[:, 0:512]), win("LN", 0, 32), more=wm("LN"))
+        act(("U2b", T.U2[:, 512:1024]), win("LN", 32, 64), more=wm("LN"))
+        if t < 2:
+            need("g", lastw["U2a"])
+            need("g", lastw["U2b"])
+            g.remote_dma_fused([RemoteDMATransfer(dst_ids=[dst(topo, h)], dma_engine_mask=1 << topo.engines(core, h)[j],
+                                                  remote_sem=T.sem["go%d" % (t + 1)]) for j, h in enumerate(mine)], local_sem=T.sem.ls)
+            nls[0] += len(mine)
+
+        def numbers():
+            ts(X("y4"), nw, float(WC), A_.is_ge, 4736.0, A_.mult)
+            ys = [("yy%d" % j, T.yy[:, 64 * j:64 * j + 64]) for j in range(3)]
+            for j, d in enumerate((2880, 576, 192)):
+                act(ys[j], nw, IDENT, scale=1.0 / d, bias=-(d - 1) / 2.0 / d)
+            for big in (12582912.0, -12582912.0):
+                for y in ys:
+                    act(y, y, IDENT, bias=big)
+            o = C("PG2", 0, 64)
+            for j, r in enumerate([nw, X("y4")] + ys):
+                w = max(0, j - 1)
+                mm(o, C("IDF", 128 * w, 128 * w + 128), r, j == 0, j == 4)
+            act(X("YO"), o)
+            dma("y", "oO%d" % t, [(T.yo[:, 64 * t:64 * t + 64], T.YO[:])], rd=["YO"])
+
+        if t == 0:
+            for j, f in enumerate((1.0, -7488.0, 1344.0, -128.0)):
+                act(C("IDF", 128 * j, 128 * j + 128), X("ID"), scale=f)
+        if t == 2:
+            numbers()
+        for hf in "ab":
+            lo = 0 if hf == "a" else 512
+            emit("v", lambda e, c=slice(lo, lo + 512): e.tensor_tensor_scan(T.SC[:, c], T.RS[:, c], T.U2[:, c], 0.0, A_.add, A_.max),
+                 [("RS", 0), ("U2" + hf, 0)], ("SC" + hf, 0))
+        tt(X("we"), C("SC", 7, None, 8), C("XW", 128 * t, 128 * t + 128), A_.max, more=[("SCa", 0), ("SCb", 0)])
+        ts(X("wh"), X("we"), -4194304.0, A_.is_lt, OFF, A_.mult)
+        tt(X("ww"), X("wh"), X("we"), A_.add)
+        act(X("wn"), X("ww"), IDENT, scale=-1.0, bias=temp)
+        tt(X("ws"), C("ww", 0, None, 2), C("ww", 1, None, 2), A_.subtract)
+        ts(X("wi"), X("ws"), 0.5, A_.mult, -0.25, A_.add)
+        if t < 2:
+            ts(X("wj"), X("ws"), -0.5, A_.mult, 0.25, A_.add)
+            tt(C(sb, 0, 64), C("wn", 1, None, 2), X("wi"), A_.min)
+            tt(C(sb, 64, 128), C("wn", 0, None, 2), X("wj"), A_.min)
+            send(t + 1, sb)
+            spread(t + 1, sb)
+            act(X("YL"), C(sb, 64, 128), scale=-1.0)
+        else:
+            act(X("wl"), C("ww", 0, None, 2), IDENT, bias=ntemp)
+            tt(C(sb, 0, 64), C("wn", 1, None, 2), X("wi"), A_.min)
+            tt(X("YL"), X("wl"), X("wi"), A_.max)
+        dma("y", "oR%d" % t, [(T.yr[:, 64 * t:64 * t + 64], T[sb][:, 0:64])], rd=[sb])
+        dma("y", "oL%d" % t, [(T.yl[:, 64 * t:64 * t + 64], T.YL[:])], rd=["YL"])
+        if t < 2:
+            lists(t + 1)
+            sels(t + 1)
+            own_walls(t + 1)
+            act(X("PP2"), C("XN", 512 * t + 512, 512 * t + 1024))
+            empties(t + 1)
+            diffs(((2, 3, 5), (6,))[t], ((2,), ())[t])
+            numbers()
+    g.wait_ge(T.sem.ls, nls[0])
+    for sem, c in cnt.items():
+        if known["g"].get(sem, 0) < c:
+            g.wait_ge(T.sem[sem], c)

@@ -6,11 +6,11 @@ A_ = AluOpType
 COPY = ActivationFunctionType.Copy
 IDENT = ActivationFunctionType.Identity
 RELU = ActivationFunctionType.Relu
+SIGN = ActivationFunctionType.Sign
 G1, R1, B1 = 2880, 576, 192
 WC = 8 * G1
 EC = 43264
 BIG = 8388608.0
-OFF = 6291456.0
 PN = [576, 192, 192]
 
 
@@ -26,18 +26,18 @@ SCRATCH = {
     "i1": _i(192), "i2": _i(192), "i3": _i(192), "f1": _f(192), "f2": _f(192), "f3": _f(192), "f4": _f(192), "CD": _f(192),
     "PI": _i(1), "pc": _i(16), "fc": _f(40), "CI": _f(176), "REL": _f(176), "tmp": _f(176), "tmp2": _f(176),
     "QF": _f(512), "QB": _b(512), "GF": _f(512), "EM": _b(176), "AD": _b(1120), "BM": _b(176), "C1": _b(144),
-    "LT": _b(128), "ID": _b(128), "IDF": _f(512), "UPC": _b(192),
+    "LT": _b(128), "SL": _b(256), "ID": _b(128), "IDF": _f(512), "UPC": _b(192),
     "j1": _i(32), "j2": _i(32), "j3": _i(32), "j4": _i(8), "j5": _i(8), "j6": _i(8), "j7": _i(8), "j8": _i(8),
-    "SEL": _u(16), "XBL": _u(32), "CDL": _u(12), "DSL": _u(8), "LU": _u(192), "LO": _u(192), "NO": _f(192),
+    "SEL": _u(16), "XBL": _u(32), "CDL": _u(12), "DSL": _u(8), "ZB": _b(128), "LU": _u(192), "LO": _u(192), "NO": _b(192),
     "XR": _f(1536), "XN": _f(1536), "XW": _f(384), "RS": _f(1024),
     "U": _f(1024), "T0": _f(1024), "T1": _f(1024), "TL": _f(1024), "D1": _f(512), "D2": _f(512),
     "IA1": _b(512), "IB1": _b(512), "IA2": _b(512), "IB2": _b(512), "VR": _b(1024), "VL": _b(1024),
     "K": _f(64), "kz": _f(64), "ky": _f(64), "kf": _f(64), "KH": _b(64), "KL": _b(64), "LKR": _u(64), "LKL": _u(64),
-    "m1": _f(64), "m2": _f(64), "GX": _b(64), "FI": _b(64), "REV": _b(64), "FH": _b(64), "FL": _b(64),
-    "DP": _f(128), "DS": _f(128), "EN": _f(128), "cz": _f(8), "cy": _f(8), "CLS": _u(8),
+    "m1": _b(64), "m2": _b(64), "GX": _b(64), "FI": _b(64), "REV": _b(64), "FH": _b(64), "FL": _b(64), "FG": _b(64),
+    "DP": _f(128), "DS": _f(128), "EN": _f(128), "CLS": _u(8),
     "o1": _f(64), "o2": _f(64), "o3": _f(64), "n1": _f(64), "nz": _f(64), "ny": _f(64), "LN": _u(64),
-    "U2": _f(1024), "SC": _f(1024), "we": _f(128), "wh": _f(128), "ww": _f(128), "wn": _f(128), "ws": _f(64), "wl": _f(64),
-    "wi": _i(64), "wj": _i(64), "YL": _f(64), "YO": _f(64), "yy": _f(192), "y4": _f(64),
+    "U2": _f(1024), "SC": _f(1024), "ww": _f(128), "wn": _f(128), "ws": _f(64), "wi": _i(128),
+    "YL": _f(64), "YO": _f(64), "yy": _f(192), "y4": _f(64),
     "PZ1": ("psum", [128, 512], "float32"), "PZ2": ("psum", [128, 512], "float32"), "PCN": ("psum", [128, 512], "float32"),
     "PPF": ("psum", [128, 512], "float32"), "PDM": ("psum", [128, 512], "float32"), "PCH": ("psum", [128, 512], "float32"),
     "PP2": ("psum", [128, 512], "float32"), "PG2": ("psum", [128, 512], "float32"),
@@ -58,12 +58,12 @@ def dst(topo, c):
 
 def plan(T, topo):
     cores = list(T.cores)
-    role, of = {}, {}
+    role, of, extra = {}, {}, []
     for r, c in enumerate(cores):
         near = [h for h in topo.cores_of(c) if topo.die(h) == topo.die(c) and h not in cores]
-        far = [h for h in topo.cores_of(c) if topo.die(h) != topo.die(c) and h not in cores]
         off = [q for q, d in enumerate(cores) if topo.chip(d) != topo.chip(c)]
-        for q, h in zip(off, near + far):
+        extra += [(r, q) for q in off[len(near):]]
+        for q, h in zip(off, near):
             role[h] = {"rank": r, "A": q, "feed": cores[q], "fwd": []}
             of[(r, q)] = h
     for (r, q), h in of.items():
@@ -72,7 +72,7 @@ def plan(T, topo):
                 if r2 != r and topo.chip(cores[r2]) == topo.chip(cores[r]) and topo.die(cores[r2]) == topo.die(cores[q]):
                     role[h]["feed"] = of[(r2, q)]
                     role[of[(r2, q)]]["fwd"].append(h)
-    return cores, role
+    return cores, role, extra
 
 
 def calls_of(info, cores):
@@ -116,7 +116,7 @@ def helper(g, core, T, topo, cores, role):
 
 
 def rank_program(g, core, T, topo):
-    cores, role = plan(T, topo)
+    cores, role, extra = plan(T, topo)
     rank = T.rank_of(core)
     if rank is None:
         if core in role:
@@ -125,8 +125,7 @@ def rank_program(g, core, T, topo):
     mine = [h for h in role if role[h]["rank"] == rank]
     near = [q for q, c in enumerate(cores) if q != rank and topo.chip(c) == topo.chip(core)]
     arr_n = sum(16 * len(calls_of(role[h], cores)) for h in mine)
-    V, S, PE, Y = g.vector, g.scalar, g.tensor, g.sync
-    Q = {"v": V, "s": S, "p": PE, "g": g, "y": Y}
+    Q = {"v": g.vector, "s": g.scalar, "p": g.tensor, "g": g, "y": g.sync}
     QS = {"v": "qv", "s": "qs", "p": "qp", "g": "qg"}
     cnt, known, lastw, readers, lastx = {}, {q: {} for q in Q}, {}, {}, {}
 
@@ -279,10 +278,11 @@ def rank_program(g, core, T, topo):
 
     def send(e, name):
         deps("g", [name], [], ())
-        offs = [h for h in role if role[h]["feed"] == core]
-        en = topo.engines(core, offs[0])
-        trs = [RemoteDMATransfer(dst_ids=[dst(topo, h) for h in offs], dma_engine_mask=pl(en), remote_sem=T.sem["fA%d" % e],
-                                 srcs=[T[name][:]], dsts=[T["DA%d" % e][0:128, :] for h in offs])]
+        offs = [(h, T["DA%d" % e][0:128, :]) for h in role if role[h]["feed"] == core]
+        offs += [(cores[r], T["NB%d" % e][:]) for r, q in extra if q == rank]
+        en = topo.engines(core, offs[0][0])
+        trs = [RemoteDMATransfer(dst_ids=[dst(topo, h) for h, _ in offs], dma_engine_mask=pl(en), remote_sem=T.sem["fA%d" % e],
+                                 srcs=[T[name][:]], dsts=[d for _, d in offs])]
         nls[0] += len(en)
         for q in near:
             e2 = [x for x in topo.engines(core, cores[q]) if x not in en]
@@ -291,7 +291,7 @@ def rank_program(g, core, T, topo):
             nls[0] += len(e2)
         g.remote_dma_fused(trs, local_sem=T.sem.ls)
 
-    def put(e, sem, name, src, rd):
+    def put(qu, e, sem, name, src, rd):
         nn = PN[e]
         c0 = src * R1 + (e - 1) * B1 * (e > 0)
         pairs = [(T.W[:, c0:c0 + nn], T[name][:])]
@@ -299,15 +299,18 @@ def rank_program(g, core, T, topo):
             c = c0 + k * G1
             pairs.append((T.W[0:128 - 16 * k, c:c + nn], T[name][16 * k:128, :]))
             pairs.append((T.W[128 - 16 * k:128, c:c + nn], T[name][0:16 * k, :]))
-        dma("y", sem + str(e), pairs, rd=rd, wr=[sem])
+        dma(qu, sem + str(e), pairs, rd=rd, wr=[sem])
 
     def spread(e, name):
+        deps("s", [], ["W"], ())
         deps("y", [], ["W"], ())
-        put(e, "own", name, rank, [name])
-        for q in near:
+        put("s", e, "own", name, rank, [name])
+        for q in near + [q for r, q in extra if r == rank]:
             h = [h for h in role if role[h]["feed"] == cores[q]][0]
-            Y.wait_ge(T.sem["fB%d" % e], len([x for x in topo.engines(cores[q], core) if x not in topo.engines(cores[q], h)]))
-            put(e, "nbd", "NB%d" % e, q, [])
+            en = topo.engines(cores[q], core)
+            Q["y"].wait_ge(T.sem["f%s%d" % ("B" if q in near else "A", e)],
+                           len([x for x in en if x not in topo.engines(cores[q], h)] if q in near else en))
+            put("y", e, "nbd", "NB%d" % e, q, [])
 
     send(0, "SB0")
     spread(0, "SB0")
@@ -336,15 +339,14 @@ def rank_program(g, core, T, topo):
     tt(X("j2"), X("j2"), X("j3"), A_.add)
     cp(X("XBL"), X("j2"))
     temp = fcol(p15, 1024.0, A_.mult)
-    tempo = fcol(temp, -OFF, A_.add)
     ntemp = fcol(temp, -1.0, A_.mult)
 
     def own_walls(t):
         b = t * B1
         act(C("XR", 512 * t, 512 * t + 512), ("SB0", T.SB0[:, b:b + 64].indirect(T.XBL[:])), more=[("XBL", 0)])
         act(C("XN", 512 * t, 512 * t + 512), ("SB0", T.SB0[:, b + 64:b + 128].indirect(T.XBL[:])), more=[("XBL", 0)])
-        act(C("XW", 128 * t, 128 * t + 128, 2), C("SB0", b + 64, b + 128), IDENT, scale=-1.0, bias=tempo)
-        act(C("XW", 128 * t + 1, 128 * t + 128, 2), C("SB0", b, b + 64), IDENT, scale=-1.0, bias=tempo)
+        act(C("XW", 128 * t, 128 * t + 64), C("SB0", b + 64, b + 128), IDENT, scale=-1.0, bias=temp)
+        act(C("XW", 128 * t + 64, 128 * t + 128), C("SB0", b, b + 64), IDENT, scale=-1.0, bias=temp)
 
     def sel2(base, col, big, full):
         x, y0, y1, y2 = newf(), newf(), newf(), newf()
@@ -423,6 +425,8 @@ def rank_program(g, core, T, topo):
     sels(0)
     own_walls(0)
     act(X("PP2"), C("XN", 0, 512))
+    for j, f in enumerate((1.0, -7488.0, 1344.0, -128.0)):
+        act(C("IDF", 128 * j, 128 * j + 128), X("ID"), scale=f)
     empties(0)
     p8f = fcol(p120, 1.0, A_.mult)
     ts(X("tmp"), X("CI"), p8f, A_.subtract)
@@ -432,21 +436,20 @@ def rank_program(g, core, T, topo):
     tt(C("tmp2", 0, 128), C("tmp2", 0, 128), C("tmp", 0, 128), A_.mult)
     ts(C("tmp", 0, 128), C("CI", 0, 128), pf, A_.is_equal, -0.5, A_.mult)
     tt(X("LT"), C("tmp2", 0, 128), C("tmp", 0, 128), A_.add)
-    HmE = fcol(H, -float(EC), A_.add)
     EH = fcol(nH, EC + 128.0, A_.add)
     s64 = fcol(p3i, 8.0, A_.mult)
     capN = fcol(s64, float(WC), A_.add)
     nHs = newf()
     tt(nHs, s64, nH, A_.add)
-    p34 = fcol(p3i, 4.0, A_.mult)
-    p347 = newf()
-    tt(p347, p34, p7, A_.add)
-    ts(C("j2", 0, 8), C("j1", 0, 8), 4, A_.bitwise_and)
-    ts(C("j3", 0, 8), C("j1", 0, 8), 3, A_.bitwise_and)
-    ts(C("j2", 0, 8), C("j2", 0, 8), 16, A_.mult, p347, A_.add)
-    ts(C("j3", 0, 8), C("j3", 0, 8), 8, A_.mult)
-    tt(C("j2", 0, 8), C("j2", 0, 8), C("j3", 0, 8), A_.add)
-    cp(X("DSL"), C("j2", 0, 8))
+    big1 = fcol(p3i, -BIG / 8, A_.mult)
+    big0 = newf()
+    ts(big0, big1, -1.0, A_.mult, -BIG, A_.add)
+    ts(C("tmp", 0, 128), C("REL", 0, 128), 0.0, A_.is_ge)
+    ts(C("tmp2", 0, 128), C("REL", 0, 128), 16.0, A_.is_lt)
+    tt(C("tmp", 0, 128), C("tmp", 0, 128), C("tmp2", 0, 128), A_.mult)
+    ts(C("SL", 0, 128), C("tmp", 0, 128), big0, A_.mult)
+    ts(C("SL", 128, 256), C("tmp", 0, 128), big1, A_.mult)
+    op("v", lambda e: e.memset(T.ZB[:], 0.0), wr=["ZB"])
 
     def win(L, lo, hi):
         return ("W", T.W[:].indirect(T[L][:, lo:hi]))
@@ -491,31 +494,49 @@ def rank_program(g, core, T, topo):
         for side in range(2):
             act(("TL%d" % side, T.TL[:, 512 * side:512 * side + 512]), win("LKL", 32 * side, 32 * side + 32), more=wm("LKL"))
             tt(C("VR", 512 * side, 512 * side + 512), win("LKR", 32 * side, 32 * side + 32), C("XR", xb, xb + 512), (A_.is_gt, A_.is_lt)[side], more=wm("LKR"))
-        act(X("kf"), X("K"), IDENT, bias=-float(EC))
-        act(X("KH"), X("kf"))
-        tt(X("m1"), C("PZ1", 0, 64), C("NO", 64 * t, 64 * t + 64), A_.max)
-        tt(X("m2"), C("PZ2", 0, 64), X("m1"), A_.max)
-        ts(X("GX"), X("m2"), 0.25, A_.is_gt)
-        for side in range(2):
-            tt(C("VL", 512 * side, 512 * side + 512), ("TL%d" % side, T.TL[:, 512 * side:512 * side + 512]), X("PP2"), (A_.is_lt, A_.is_gt)[side])
-        tt(X("KL"), X("kf"), X("KH"), A_.subtract)
         o = C("PCN", 0, 64)
         for i in range(16):
             mm(o, C("EM", 24 - i, 152 - i), C("VR", i, None, 16), i == 0, False)
-        mm(o, X("ID"), X("GX"), False, False)
-        for i in range(16):
-            mm(o, C("EM", 24 - i, 152 - i), C("VL", i, None, 16), False, i == 15)
+        mm(C("PDM", 0, 128), X("ID"), X("ZB"), True, False)
+        for par in range(2):
+            for side in range(2):
+                c = slice(512 * side + par, 512 * side + 512, 2)
+                tt(("VL%d" % par, T.VL[:, c]), ("TL%d" % side, T.TL[:, c]), C("PP2", par, 512, 2), (A_.is_lt, A_.is_gt)[side])
+        if t == 0:
+            p34 = fcol(p3i, 4.0, A_.mult)
+            p347 = newf()
+            tt(p347, p34, p7, A_.add)
+            ts(C("j2", 0, 8), C("j1", 0, 8), 4, A_.bitwise_and)
+            ts(C("j3", 0, 8), C("j1", 0, 8), 3, A_.bitwise_and)
+            ts(C("j2", 0, 8), C("j2", 0, 8), 16, A_.mult, p347, A_.add)
+            ts(C("j3", 0, 8), C("j3", 0, 8), 8, A_.mult)
+            tt(C("j2", 0, 8), C("j2", 0, 8), C("j3", 0, 8), A_.add)
+            cp(X("DSL"), C("j2", 0, 8))
+        for z in (1, 2):
+            act(X("m%d" % z), C("PZ%d" % z, 0, 64), RELU, bias=-0.25)
+        o = C("PZ1", 64, 128)
+        mm(o, X("ID"), C("NO", 64 * t, 64 * t + 64), True, False)
+        mm(o, X("ID"), X("m1"), False, False)
+        mm(o, X("ID"), X("m2"), False, True)
+        act(X("kf"), X("ky"), IDENT, bias=-float(EC))
+        act(X("KH"), X("kf"))
+        act(X("GX"), o, SIGN)
+        tt(X("KL"), X("kf"), X("KH"), A_.subtract)
+        o = C("PCN", 0, 64)
+        for i in list(range(0, 16, 2)) + list(range(1, 16, 2)):
+            mm(o, C("EM", 24 - i, 152 - i), ("VL%d" % (i % 2), T.VL[:, i::16]), False, False)
+        mm(o, X("ID"), X("GX"), False, True)
+        dm = [(C("PDM", 64 * side + 32 * a, 64 * side + 32 * a + 32), C("QB", 128 * (2 * a + side), 128 * (2 * a + side) + 128), 32 * side)
+              for side in range(2) for a in range(2)]
+        for oo, l, w in dm:
+            mm(oo, l, C("GX", w, w + 32), False, False)
         ts(X("REV"), o, 0.0, A_.is_equal)
         mm(C("PPF", 0, 64), X("LT"), X("REV"), True, True)
         ts(X("FI"), C("PPF", 0, 64), 0.0, A_.is_lt)
         tt(X("FH"), X("FI"), X("KH"), A_.mult)
         tt(X("FL"), X("FI"), X("KL"), A_.mult)
-        for side in range(2):
-            for a in range(2):
-                oo = C("PDM", 64 * side + 32 * a, 64 * side + 32 * a + 32)
-                l = C("QB", 128 * (2 * a + side), 128 * (2 * a + side) + 128)
-                mm(oo, l, C("GX", 32 * side, 32 * side + 32), True, False)
-                mm(oo, l, C("FI", 32 * side, 32 * side + 32), False, True)
+        for j, (oo, l, w) in enumerate(dm):
+            mm(oo, l, C("FI", w, w + 32), False, j == 3)
         o = C("PCH", 0, 8)
         for x in ("FH", "FL"):
             for c in range(8):
@@ -525,9 +546,11 @@ def rank_program(g, core, T, topo):
         act(X("DS"), ("DP", T.DP[:].indirect(T.DSL[:])), more=[("DSL", 0)])
         tt(X("o1"), C("DS", 0, 64), C("DS", 64, 128), A_.add)
         tt(X("o2"), X("o1"), oc, A_.mult)
-        ts(X("cz"), o, HmE, A_.is_lt, float(WC), A_.mult)
-        tt(X("cy"), X("cz"), o, A_.add)
-        ts(X("CLS"), X("cy"), EH, A_.add, float(WC + 128), A_.min)
+        ts(X("CLS"), o, EH, A_.add, float(WC + 128), A_.min)
+        sides = (("PPF", 0), ("PCH", 1))
+        for b, side in sides:
+            w = 128 * t + 64 * side
+            mm(C(b, 64, 128), C("IDF", 0, 128), C("XW", w, w + 64), True, False)
         tt(X("o3"), oc, X("o2"), A_.subtract)
         tt(X("EN"), win("CLS", 0, 8), X("DS"), A_.mult, more=wm("CLS"))
         tt(X("n1"), C("EN", 0, 64), C("EN", 64, 128), A_.add)
@@ -537,8 +560,11 @@ def rank_program(g, core, T, topo):
         ts(X("nz"), nw, H, A_.is_lt, float(WC), A_.mult)
         tt(X("ny"), X("nz"), nw, A_.add)
         ts(X("LN"), X("ny"), nHs, A_.add, capN, A_.min)
-        cp(("U2a", T.U2[:, 0:512]), win("LN", 0, 32), more=wm("LN"))
-        act(("U2b", T.U2[:, 512:1024]), win("LN", 32, 64), more=wm("LN"))
+        cp(("U2a", T.U2[:, 0:384]), win("LN", 0, 24), more=wm("LN"))
+        act(("U2b", T.U2[:, 384:1024]), win("LN", 24, 64), more=wm("LN"))
+        act(X("FG"), nw, IDENT, scale=-1.0, bias=float(EC))
+        for b, side in sides:
+            mm(C(b, 64, 128), C("SL", 128 * side, 128 * side + 128), X("FG"), False, True)
         if t < 2:
             need("g", lastw["U2a"])
             need("g", lastw["U2b"])
@@ -561,32 +587,26 @@ def rank_program(g, core, T, topo):
             act(X("YO"), o)
             dma("y", "oO%d" % t, [(T.yo[:, 64 * t:64 * t + 64], T.YO[:])], rd=["YO"])
 
-        if t == 0:
-            for j, f in enumerate((1.0, -7488.0, 1344.0, -128.0)):
-                act(C("IDF", 128 * j, 128 * j + 128), X("ID"), scale=f)
         if t == 2:
             numbers()
-        for hf in "ab":
-            lo = 0 if hf == "a" else 512
-            emit("v", lambda e, c=slice(lo, lo + 512): e.tensor_tensor_scan(T.SC[:, c], T.RS[:, c], T.U2[:, c], 0.0, A_.add, A_.max),
+        for hf, lo, hi in (("a", 0, 384), ("b", 384, 1024)):
+            emit("v", lambda e, c=slice(lo, hi): e.tensor_tensor_scan(T.SC[:, c], T.RS[:, c], T.U2[:, c], 0.0, A_.add, A_.max),
                  [("RS", 0), ("U2" + hf, 0)], ("SC" + hf, 0))
-        tt(X("we"), C("SC", 7, None, 8), C("XW", 128 * t, 128 * t + 128), A_.max, more=[("SCa", 0), ("SCb", 0)])
-        ts(X("wh"), X("we"), -4194304.0, A_.is_lt, OFF, A_.mult)
-        tt(X("ww"), X("wh"), X("we"), A_.add)
-        act(X("wn"), X("ww"), IDENT, scale=-1.0, bias=temp)
-        tt(X("ws"), C("ww", 0, None, 2), C("ww", 1, None, 2), A_.subtract)
-        ts(X("wi"), X("ws"), 0.5, A_.mult, -0.25, A_.add)
+        for b, side in sides:
+            tt(C("ww", 64 * side, 64 * side + 64), C("SC", 7 + 8 * side, None, 16), C(b, 64, 128), A_.max, more=[("SCa", 0), ("SCb", 0)])
+        act(C("wn", 0, 64), C("ww", 64, 128), IDENT, scale=-1.0, bias=temp)
+        act(C("wn", 64, 128), C("ww", 0, 64), IDENT, scale=-1.0 if t < 2 else 1.0, bias=temp if t < 2 else ntemp)
+        tt(X("ws"), C("ww", 0, 64), C("ww", 64, 128), A_.subtract)
+        ts(C("wi", 0, 64), X("ws"), 0.5, A_.mult, -0.25, A_.add)
         if t < 2:
-            ts(X("wj"), X("ws"), -0.5, A_.mult, 0.25, A_.add)
-            tt(C(sb, 0, 64), C("wn", 1, None, 2), X("wi"), A_.min)
-            tt(C(sb, 64, 128), C("wn", 0, None, 2), X("wj"), A_.min)
+            ts(C("wi", 64, 128), X("ws"), -0.5, A_.mult, 0.25, A_.add)
+            tt(C(sb, 0, 128), X("wn"), X("wi"), A_.min)
             send(t + 1, sb)
             spread(t + 1, sb)
             act(X("YL"), C(sb, 64, 128), scale=-1.0)
         else:
-            act(X("wl"), C("ww", 0, None, 2), IDENT, bias=ntemp)
-            tt(C(sb, 0, 64), C("wn", 1, None, 2), X("wi"), A_.min)
-            tt(X("YL"), X("wl"), X("wi"), A_.max)
+            tt(C(sb, 0, 64), C("wn", 0, 64), C("wi", 0, 64), A_.min)
+            tt(X("YL"), C("wn", 64, 128), C("wi", 0, 64), A_.max)
         dma("y", "oR%d" % t, [(T.yr[:, 64 * t:64 * t + 64], T[sb][:, 0:64])], rd=[sb])
         dma("y", "oL%d" % t, [(T.yl[:, 64 * t:64 * t + 64], T.YL[:])], rd=["YL"])
         if t < 2:

import numpy as np
from concourse.bass import DstId, RemoteDMATransfer
from concourse.mybir import dt, AluOpType, AxisListType, ActivationFunctionType

A_ = AluOpType
COPY = ActivationFunctionType.Copy
IDENT = ActivationFunctionType.Identity
RELU = ActivationFunctionType.Relu
SIGN = ActivationFunctionType.Sign
G1, R1, B1 = 2880, 576, 192
WC = 8 * G1
EC = 43264
BIG = 8388608.0
PN = [576, 192, 192]


def _f(n): return ("sbuf", [128, n], "float32")
def _i(n): return ("sbuf", [128, n], "int32")
def _b(n): return ("sbuf", [128, n], "bfloat16")
def _u(n): return ("sbuf", [128, n], "uint16")


SCRATCH = {
    "W": _f(WC + B1), "LI": _i(192), "RI": _i(192), "OI": _i(192),
    "SB0": _f(576), "SB1": _f(192), "SB2": _f(192), "SB3": _f(192), "NB0": _f(576), "NB1": _f(192), "NB2": _f(192),
    "i1": _i(192), "i2": _i(192), "i3": _i(192), "f1": _f(192), "f2": _f(192), "f3": _f(192), "f4": _f(192), "CD": _f(192),
    "PI": _i(1), "pc": _i(16), "fc": _f(40), "CI": _f(176), "REL": _f(176), "tmp": _f(176), "tmp2": _f(176),
    "QF": _f(512), "QB": _b(512), "GF": _f(512), "EM": _b(176), "AD": _b(1120), "BM": _b(176), "C1": _b(144),
    "LT": _b(128), "SL": _b(256), "ID": _b(128), "IDF": _f(512), "UPC": _b(192),
    "j1": _i(32), "j2": _i(32), "j3": _i(32), "j4": _i(8), "j5": _i(8), "j6": _i(8), "j7": _i(8), "j8": _i(8),
    "SEL": _u(16), "XBL": _u(32), "CDL": _u(12), "DSL": _u(8), "ZB": _b(128), "LU": _u(192), "LO": _u(192), "NO": _b(192),
    "XR": _f(1536), "XN": _f(1536), "XW": _f(384), "RS": _f(1024),
    "U": _f(1024), "T0": _f(1024), "T1": _f(1024), "TL": _f(1024), "D1": _f(512), "D2": _f(512),
    "IA1": _b(512), "IB1": _b(512), "IA2": _b(512), "IB2": _b(512), "VR": _b(1024), "VL": _b(1024),
    "K": _f(64), "kz": _f(64), "ky": _f(64), "kf": _f(64), "KH": _b(64), "KL": _b(64), "LKR": _u(64), "LKL": _u(64),
    "m1": _b(64), "m2": _b(64), "GX": _b(64), "FI": _b(64), "REV": _b(64), "FH": _b(64), "FL": _b(64), "FG": _b(64),
    "DP": _f(128), "DS": _f(128), "EN": _f(128), "CLS": _u(8),
    "o1": _f(64), "o2": _f(64), "o3": _f(64), "n1": _f(64), "nz": _f(64), "ny": _f(64), "LN": _u(64),
    "U2": _f(1024), "SC": _f(1024), "ww": _f(128), "wn": _f(128), "ws": _f(64), "wi": _i(128),
    "YL": _f(64), "YO": _f(64), "yy": _f(192), "y4": _f(64),
    "PZ1": ("psum", [128, 512], "float32"), "PZ2": ("psum", [128, 512], "float32"), "PCN": ("psum", [128, 512], "float32"),
    "PPF": ("psum", [128, 512], "float32"), "PDM": ("psum", [128, 512], "float32"), "PCH": ("psum", [128, 512], "float32"),
    "PP2": ("psum", [128, 512], "float32"), "PG2": ("psum", [128, 512], "float32"),
    "DA0": ("dram", [256, 576], "float32"), "DA1": ("dram", [256, 192], "float32"), "DA2": ("dram", [256, 192], "float32"),
}
SEMAPHORES = ["qv", "qs", "qp", "qg", "ls", "ldO", "ldL", "ldR", "go1", "go2"] + [
    "%s%d" % (k, e) for k in ("arr", "own", "nbd", "fA", "fB", "dA", "oO", "oR", "oL") for e in range(3)]


def pl(bits):
    return sum(1 << b for b in bits)


def dst(topo, c):
    rid, pid, _ = topo.addr(c)
    return DstId(rid=rid, pnc=pid)


def plan(T, topo):
    cores = list(T.cores)
    role, of, extra = {}, {}, []
    for r, c in enumerate(cores):
        near = [h for h in topo.cores_of(c) if topo.die(h) == topo.die(c) and h not in cores]
        off = [q for q, d in enumerate(cores) if topo.chip(d) != topo.chip(c)]
        extra += [(r, q) for q in off[len(near):]]
        for q, h in zip(off, near):
            role[h] = {"rank": r, "A": q, "feed": cores[q], "fwd": []}
            of[(r, q)] = h
    for (r, q), h in of.items():
        if topo.die(cores[r]) != topo.die(cores[q]):
            for r2 in range(len(cores)):
                if r2 != r and topo.chip(cores[r2]) == topo.chip(cores[r]) and topo.die(cores[r2]) == topo.die(cores[q]):
                    role[h]["feed"] = of[(r2, q)]
                    role[of[(r2, q)]]["fwd"].append(h)
    return cores, role, extra


def calls_of(info, cores):
    if info["feed"] in cores:
        return [[0], [1, 2, 3, 4], [5, 6], [7]]
    return [[0, 1, 2, 3, 4, 5, 6, 7]]


def helper(g, core, T, topo, cores, role):
    info = role[core]
    rc = cores[info["rank"]]
    eng = topo.engines(core, rc)
    direct = info["feed"] in cores
    ls = 0
    for e in range(3):
        n, buf, fa = PN[e], T["DA%d" % e], T.sem["fA%d" % e]
        got = len(topo.engines(info["feed"], core)) * (1 if direct else 2)
        g.wait_ge(fa, got)
        if direct:
            g.sync.wait_ge(fa, got)
            g.sync.dma_start(buf[128:240, :], buf[0:112, :]).then_inc(T.sem["dA%d" % e], 16)
        for h in info["fwd"]:
            en = topo.engines(core, h)
            g.remote_dma_fused([RemoteDMATransfer(dst_ids=[dst(topo, h)] * 2, dma_engine_mask=pl(en), remote_sem=fa,
                                                  srcs=[buf[0:128, :]], dsts=[buf[0:128, :], buf[128:256, :]])], local_sem=T.sem.ls)
            ls += len(en)
        if e:
            g.wait_ge(T.sem["go%d" % e], 1)
        for ci, call in enumerate(calls_of(info, cores)):
            if ci == 1:
                g.wait_ge(T.sem["dA%d" % e], 16)
            w = len(eng) // len(call)
            trs = []
            for j, k in enumerate(call):
                c0 = k * G1 + info["A"] * R1 + (e - 1) * B1 * (e > 0)
                trs.append(RemoteDMATransfer(dst_ids=[dst(topo, rc)], dma_engine_mask=pl(eng[j * w:(j + 1) * w]), remote_sem=T.sem["arr%d" % e],
                                             srcs=[buf[16 * k:16 * k + 128, :]], dsts=[T.W[:, c0:c0 + n]]))
                ls += w
            g.remote_dma_fused(trs, local_sem=T.sem.ls)
    g.wait_ge(T.sem.ls, ls)


def rank_program(g, core, T, topo):
    cores, role, extra = plan(T, topo)
    rank = T.rank_of(core)
    if rank is None:
        if core in role:
            helper(g, core, T, topo, cores, role)
        return
    mine = [h for h in role if role[h]["rank"] == rank]
    near = [q for q, c in enumerate(cores) if q != rank and topo.chip(c) == topo.chip(core)]
    arr_n = sum(16 * len(calls_of(role[h], cores)) for h in mine)
    Q = {"v": g.vector, "s": g.scalar, "p": g.tensor, "g": g, "y": g.sync}
    QS = {"v": "qv", "s": "qs", "p": "qp", "g": "qg"}
    cnt, known, lastw, readers, lastx = {}, {q: {} for q in Q}, {}, {}, {}

    def need(q, tok):
        _, sem, c, clock = tok
        if known[q].get(sem, 0) >= c:
            return
        Q[q].wait_ge(T.sem[sem], c)
        for s2, c2 in clock.items():
            known[q][s2] = max(known[q].get(s2, 0), c2)
        known[q][sem] = max(known[q].get(sem, 0), c)

    def deps(q, rd, wr, ps):
        toks = []
        for k in rd:
            if k in lastw:
                toks.append(lastw[k])
        for k in wr:
            if k in lastw:
                toks.append(lastw[k])
            toks += readers.get(k, [])
        for k in ps:
            if k in lastx:
                toks += [t for t in lastx[k].values() if t[0] != q]
        best = {}
        for t in toks:
            if q == "p" and t[0] == "p":
                continue
            if t[1] not in best or best[t[1]][2] < t[2]:
                best[t[1]] = t
        for t in sorted(best.values(), key=lambda t: -t[2]):
            need(q, t)

    def note(q, rd, wr, ps, tok):
        for k in rd:
            readers.setdefault(k, [])
            readers[k] = [t for t in readers[k] if not (t[0] == q and t[1] == tok[1])] + [tok]
        for k in wr:
            lastw[k] = tok
            readers[k] = []
        for k in ps:
            lastx.setdefault(k, {})
            lastx[k][q] = tok

    def op(q, fn, rd=(), wr=(), ps=()):
        deps(q, rd, wr, ps)
        sem = QS[q]
        c = cnt.get(sem, 0) + 1
        cnt[sem] = c
        fn(Q[q]).then_inc(T.sem[sem], 1)
        clock = dict(known[q])
        clock[sem] = c
        note(q, rd, wr, ps, (q, sem, c, clock))

    def dma(q, sem, pairs, rd=(), wr=()):
        deps(q, rd, wr, ())
        for o, i in pairs:
            Q[q].dma_start(o, i).then_inc(T.sem[sem], 16)
        cnt[sem] = cnt.get(sem, 0) + 16 * len(pairs)
        clock = dict(known[q])
        clock[sem] = cnt[sem]
        note(q, rd, wr, (), (q, sem, cnt[sem], clock))

    def split(xs):
        ks = [x[0] for x in xs if isinstance(x, tuple)]
        return [k for k in ks if k[0] != "P" or k == "PI"], [k for k in ks if k[0] == "P" and k != "PI"]

    def raw(x):
        return x[1] if isinstance(x, tuple) else x

    def emit(q, fn, ins, out):
        r, rp = split(ins)
        w, wp = split([out])
        return op(q, fn, r, w, rp + wp)

    def ts(out, a, s1, o1, s2=None, o2=None):
        if o2 is None:
            return emit("v", lambda e: e.tensor_scalar(raw(out), raw(a), raw(s1), None, o1), [a, s1], out)
        return emit("v", lambda e: e.tensor_scalar(raw(out), raw(a), raw(s1), raw(s2), o1, o2), [a, s1, s2], out)

    def tt(out, a, b, o, more=()):
        return emit("v", lambda e: e.tensor_tensor(raw(out), raw(a), raw(b), o), [a, b] + list(more), out)

    def cp(out, a, more=()):
        return emit("v", lambda e: e.tensor_copy(raw(out), raw(a)), [a] + list(more), out)

    def act(out, a, f=COPY, scale=1.0, more=(), bias=0.0):
        return emit("s", lambda e: e.activation(raw(out), raw(a), f, bias=raw(bias), scale=scale), [a, bias] + list(more), out)

    def mm(out, l, r, start, stop):
        return emit("p", lambda e: e.matmul(raw(out), raw(l), raw(r), start, stop), [l, r], out)

    def C(name, a, b=None, st=None):
        return (name, T[name][:, a:b:st])

    def X(name):
        return (name, T[name][:])

    dma("y", "ldO", [(T.OI[:], T.opts[:])], wr=["OI"])
    dma("y", "ldR", [(T.RI[:], T.rw[:])], wr=["RI"])
    dma("y", "ldL", [(T.LI[:], T.lw[:])], wr=["LI"])
    op("g", lambda e: e.iota(T.PI[:], [[0, 1]], 0, 1), wr=["PI"])
    op("g", lambda e: e.iota(T.j1[:], [[1, 32]], 0, 0), wr=["j1"])
    op("g", lambda e: e.iota(T.CI[:], [[1, 176]], 0, 0, allow_small_or_imprecise_dtypes=True), wr=["CI"])
    npc, nfc, nls = [0], [0], [0]

    def icol(shop, val):
        k = npc[0]
        npc[0] += 1
        o = ("pc%d" % k, T.pc[:, k:k + 1])
        ts(o, X("PI"), val, shop)
        return o

    def newf():
        k = nfc[0]
        nfc[0] += 1
        return ("fc%d" % k, T.fc[:, k:k + 1])

    def fcol(a, s1, o1):
        o = newf()
        ts(o, a, s1, o1)
        return o

    hh = icol(A_.logical_shift_right, 4)
    p3i = icol(A_.bitwise_and, 8)
    p4i = icol(A_.bitwise_and, 16)
    p15 = icol(A_.bitwise_and, 15)
    p7 = icol(A_.bitwise_and, 7)
    pg = icol(A_.bitwise_and, 96)
    p120 = icol(A_.bitwise_and, 120)
    ub = {1: icol(A_.bitwise_and, 1), 2: icol(A_.bitwise_and, 2), 4: icol(A_.bitwise_and, 4)}
    H = fcol(hh, float(G1), A_.mult)
    nH = fcol(hh, -float(G1), A_.mult)
    n = X("OI")
    ts(X("i1"), n, 1.0 / 192, A_.mult, -95.5 / 192, A_.add)
    ts(X("i2"), n, 1.0 / 1536, A_.mult, -767.5 / 1536, A_.add)
    ts(X("i3"), n, 1.0 / 64, A_.mult, -31.5 / 64, A_.add)
    ts(X("f4"), n, 7680, A_.is_ge, EC - 2880.0, A_.mult)
    ts(X("f1"), X("i1"), 2304, A_.mult)
    ts(X("f2"), X("i2"), -22464, A_.mult)
    ts(X("f3"), X("i3"), 128, A_.mult)
    tt(X("f4"), X("f4"), n, A_.add)
    tt(X("f1"), X("f1"), X("f2"), A_.add)
    tt(X("f3"), X("f3"), X("f4"), A_.add)
    for t in range(3):
        b, w = t * B1, 64 * t
        tt(C("SB0", b + 128, b + 192), C("f1", w, w + 64), C("f3", w, w + 64), A_.add)
        cp(C("SB0", b, b + 64), C("RI", w, w + 64))
        ts(C("SB0", b + 64, b + 128), C("LI", w, w + 64), -1.0, A_.mult)

    def send(e, name):
        deps("g", [name], [], ())
        offs = [(h, T["DA%d" % e][0:128, :]) for h in role if role[h]["feed"] == core]
        offs += [(cores[r], T["NB%d" % e][:]) for r, q in extra if q == rank]
        en = topo.engines(core, offs[0][0])
        trs = [RemoteDMATransfer(dst_ids=[dst(topo, h) for h, _ in offs], dma_engine_mask=pl(en), remote_sem=T.sem["fA%d" % e],
                                 srcs=[T[name][:]], dsts=[d for _, d in offs])]
        nls[0] += len(en)
        for q in near:
            e2 = [x for x in topo.engines(core, cores[q]) if x not in en]
            trs.append(RemoteDMATransfer(dst_ids=[dst(topo, cores[q])], dma_engine_mask=pl(e2), remote_sem=T.sem["fB%d" % e],
                                         srcs=[T[name][:]], dsts=[T["NB%d" % e][:]]))
            nls[0] += len(e2)
        g.remote_dma_fused(trs, local_sem=T.sem.ls)

    def put(qu, e, sem, name, src, rd):
        nn = PN[e]
        c0 = src * R1 + (e - 1) * B1 * (e > 0)
        pairs = [(T.W[:, c0:c0 + nn], T[name][:])]
        for k in range(1, 8):
            c = c0 + k * G1
            pairs.append((T.W[0:128 - 16 * k, c:c + nn], T[name][16 * k:128, :]))
            pairs.append((T.W[128 - 16 * k:128, c:c + nn], T[name][0:16 * k, :]))
        dma(qu, sem + str(e), pairs, rd=rd, wr=[sem])

    def spread(e, name):
        deps("s", [], ["W"], ())
        deps("y", [], ["W"], ())
        put("s", e, "own", name, rank, [name])
        for q in near + [q for r, q in extra if r == rank]:
            h = [h for h in role if role[h]["feed"] == cores[q]][0]
            en = topo.engines(cores[q], core)
            Q["y"].wait_ge(T.sem["f%s%d" % ("B" if q in near else "A", e)],
                           len([x for x in en if x not in topo.engines(cores[q], h)] if q in near else en))
            put("y", e, "nbd", "NB%d" % e, q, [])

    send(0, "SB0")
    spread(0, "SB0")
    op("g", lambda e: e.iota(T.RS[:], [[0, 1024]], 0, 0, allow_small_or_imprecise_dtypes=True), wr=["RS"])
    op("g", lambda e: e.affine_select(T.RS[:], T.RS[:], [[0, 128], [1, 8]], A_.not_equal, -2.0 ** 25, 0, 0), rd=["RS"], wr=["RS"])
    nH64 = fcol(nH, 64.0, A_.add)
    nH128 = fcol(nH, 128.0, A_.add)
    p15f = fcol(p15, 1.0, A_.mult)
    p3f = fcol(p3i, 1.0, A_.mult)
    pf = fcol(X("PI"), 1.0, A_.mult)
    j5 = X("j5")
    ts(j5, C("j1", 0, 8), 16, A_.mult, p15f, A_.add)
    ts(X("j6"), j5, 5, A_.logical_shift_right)
    ts(X("j7"), j5, 24, A_.bitwise_and)
    ts(X("j8"), j5, 7, A_.bitwise_and)
    ts(X("j6"), X("j6"), 192, A_.mult, 128, A_.add)
    ts(X("j7"), X("j7"), 2, A_.mult)
    tt(X("j8"), X("j8"), X("j6"), A_.add)
    tt(X("j8"), X("j8"), X("j7"), A_.add)
    cp(C("CDL", 0, 6), C("j8", 0, 6))
    ts(C("CDL", 6, 12), C("j8", 0, 6), 8, A_.add)
    act(X("CD"), ("SB0", T.SB0[:].indirect(T.CDL[:])), more=[("CDL", 0)])
    ts(X("j2"), X("j1"), 24, A_.bitwise_and)
    ts(X("j3"), X("j1"), 7, A_.bitwise_and)
    ts(X("j2"), X("j2"), 2, A_.mult, p3f, A_.add)
    tt(X("j2"), X("j2"), X("j3"), A_.add)
    cp(X("XBL"), X("j2"))
    temp = fcol(p15, 1024.0, A_.mult)
    ntemp = fcol(temp, -1.0, A_.mult)

    def own_walls(t):
        b = t * B1
        act(C("XR", 512 * t, 512 * t + 512), ("SB0", T.SB0[:, b:b + 64].indirect(T.XBL[:])), more=[("XBL", 0)])
        act(C("XN", 512 * t, 512 * t + 512), ("SB0", T.SB0[:, b + 64:b + 128].indirect(T.XBL[:])), more=[("XBL", 0)])
        act(C("XW", 128 * t, 128 * t + 64), C("SB0", b + 64, b + 128), IDENT, scale=-1.0, bias=temp)
        act(C("XW", 128 * t + 64, 128 * t + 128), C("SB0", b, b + 64), IDENT, scale=-1.0, bias=temp)

    def sel2(base, col, big, full):
        x, y0, y1, y2 = newf(), newf(), newf(), newf()
        ts(x, col, big, A_.mult)
        tt(y0, base, x, A_.add)
        tt(y1, base, x, A_.subtract)
        ts(y2, y1, full, A_.add)
        return y0, y2

    A3 = sel2(pf, p3i, 125.0, 1000.0)
    for a in range(2):
        for b in range(2):
            o = 128 * (2 * a + b)
            ts(C("QF", o, o + 128), C("CI", 0, 128), -8.0 * (b - a), A_.add, A3[a], A_.is_equal)
    act(X("QB"), X("QF"))
    gb = fcol(p3i, 2.0, A_.mult)
    gc, gd = newf(), newf()
    tt(gc, gb, pg, A_.add)
    tt(gd, gc, p7, A_.add)
    A4 = sel2(gd, p4i, 100.0, 1600.0)
    for b in range(2):
        for a in range(2):
            o = 128 * (2 * b + a)
            ts(C("GF", o, o + 128), C("CI", 0, 128), -8.0 * a, A_.add, A4[b], A_.is_equal)
    for bank, M in (("PP2", "QF"), ("PG2", "GF")):
        for x in range(2):
            for a in range(2):
                o = 128 * (2 * x + a)
                mm(C(bank, 96 * x, 96 * x + 96), C(M, o, o + 128), C("CD", 96 * a, 96 * a + 96), a == 0, a == 1)
    op("v", lambda e: e.memset(T.W[:, WC:WC + 128], -BIG), wr=["Wemp"])
    op("v", lambda e: e.memset(T.W[:, WC + 128:WC + 192], float(EC)), wr=["Wemp"])
    ts(X("f1"), C("PP2", 0, 192), H, A_.is_lt, float(WC), A_.mult)
    tt(X("f2"), X("f1"), C("PP2", 0, 192), A_.add)
    ts(X("f3"), C("PG2", 0, 192), H, A_.is_lt, float(WC), A_.mult)
    tt(X("f4"), X("f3"), C("PG2", 0, 192), A_.add)

    def lists(t):
        for side in range(2):
            i, o = 96 * side + 32 * t, 64 * t + 32 * side
            ts(C("LU", o, o + 32), C("f2", i, i + 32), nH64 if side else nH, A_.add, float(WC + 64 * side), A_.min)
        for b in range(2):
            ts(C("LO", 64 * t + b, 64 * t + 64, 2), C("f4", 96 * b + 32 * t, 96 * b + 32 * t + 32), nH128, A_.add, float(WC + 128), A_.min)

    def empties(t):
        for side in range(2):
            i, o = 96 * side + 32 * t, 64 * t + 32 * side
            ts(C("NO", o, o + 32), C("f2", i, i + 32), EC - 32.0, A_.is_ge)

    lists(0)
    h16 = fcol(hh, 16.0, A_.mult)
    ts(X("REL"), X("CI"), h16, A_.subtract)
    ts(X("EM"), X("REL"), 24.0, A_.is_equal)
    act(X("BM"), X("EM"), scale=-2.0 ** 30)

    def diffs(ds, hbs):
        for d in ds:
            tt(C("AD", 160 * d, 160 * d + 160), C("EM", 8, 168), C("EM", 8 - d, 168 - d), A_.subtract)
        for hb in hbs:
            u = fcol(ub[hb], 0.5 / hb, A_.mult)
            ts(C("UPC", 64 * (hb // 2), 64 * (hb // 2) + 64), C("CI", 0, 64), 0.0, A_.mult, u, A_.add)

    ts(X("ID"), C("CI", 0, 128), pf, A_.is_equal)
    diffs((1, 4), (1, 4))
    ts(X("j6"), j5, 31, A_.bitwise_and)
    ts(X("j7"), j5, 5, A_.logical_shift_right)
    ts(X("j6"), X("j6"), 32, A_.mult, 8, A_.add)
    ts(X("j7"), X("j7"), 8, A_.mult)
    tt(X("j6"), X("j6"), X("j7"), A_.add)

    def sels(t):
        ts(X("j4"), j5, t, A_.add)
        ts(X("j4"), X("j4"), 7, A_.bitwise_and)
        tt(X("j4"), X("j4"), X("j6"), A_.add)
        cp(C("SEL", 4 * t, 4 * t + 4), C("j4", 0, 4))

    sels(0)
    own_walls(0)
    act(X("PP2"), C("XN", 0, 512))
    for j, f in enumerate((1.0, -7488.0, 1344.0, -128.0)):
        act(C("IDF", 128 * j, 128 * j + 128), X("ID"), scale=f)
    empties(0)
    p8f = fcol(p120, 1.0, A_.mult)
    ts(X("tmp"), X("CI"), p8f, A_.subtract)
    ts(X("C1"), C("tmp", 0, 144), 8.0, A_.is_equal)
    ts(C("tmp2", 0, 128), C("tmp", 0, 128), 8.0, A_.is_lt)
    ts(C("tmp", 0, 128), C("CI", 0, 128), pf, A_.is_gt)
    tt(C("tmp2", 0, 128), C("tmp2", 0, 128), C("tmp", 0, 128), A_.mult)
    ts(C("tmp", 0, 128), C("CI", 0, 128), pf, A_.is_equal, -0.5, A_.mult)
    tt(X("LT"), C("tmp2", 0, 128), C("tmp", 0, 128), A_.add)
    EH = fcol(nH, EC + 128.0, A_.add)
    s64 = fcol(p3i, 8.0, A_.mult)
    capN = fcol(s64, float(WC), A_.add)
    nHs = newf()
    tt(nHs, s64, nH, A_.add)
    big1 = fcol(p3i, -BIG / 8, A_.mult)
    big0 = newf()
    ts(big0, big1, -1.0, A_.mult, -BIG, A_.add)
    ts(C("tmp", 0, 128), C("REL", 0, 128), 0.0, A_.is_ge)
    ts(C("tmp2", 0, 128), C("REL", 0, 128), 16.0, A_.is_lt)
    tt(C("tmp", 0, 128), C("tmp", 0, 128), C("tmp2", 0, 128), A_.mult)
    ts(C("SL", 0, 128), C("tmp", 0, 128), big0, A_.mult)
    ts(C("SL", 128, 256), C("tmp", 0, 128), big1, A_.mult)
    op("v", lambda e: e.memset(T.ZB[:], 0.0), wr=["ZB"])

    def win(L, lo, hi):
        return ("W", T.W[:].indirect(T[L][:, lo:hi]))

    def wm(L):
        return [(L, 0), ("own", 0), ("nbd", 0), ("Wemp", 0)]

    for t in range(3):
        xb = 512 * t
        for q in "vs":
            Q[q].wait_ge(T.sem["arr%d" % t], arr_n)
        cp(("Ua", T.U[:, 0:512]), win("LU", 64 * t, 64 * t + 32), more=wm("LU"))
        act(("Ub", T.U[:, 512:1024]), win("LU", 64 * t + 32, 64 * t + 64), more=wm("LU"))
        act(X("T0"), win("LO", 64 * t, 64 * t + 64), more=wm("LO"))
        for z, k in enumerate((1 + t % 7, 1 + (t + 3) % 7)):
            D, IA, IB, PZ = "D%d" % (z + 1), "IA%d" % (z + 1), "IB%d" % (z + 1), "PZ%d" % (z + 1)
            hb = 4 if k >= 4 else 2 if k >= 2 else 1
            m = 4 // hb
            off, where = 0, {}
            for r in range(2 * hb):
                if r & hb:
                    continue
                tt((D, T[D][:, off:off + 128 * m]), ("Ua", T.U[:, r ^ k::2 * hb]), ("Ub", T.U[:, r::2 * hb]), A_.subtract)
                for i in range(m):
                    where[r + 2 * hb * i] = off + i
                off += 128 * m
            act(X(IA), X(D), RELU)
            act(X(IB), X(D), RELU, scale=-1.0)
            o = C(PZ, 0, 64)
            mm(o, X("ID"), C("UPC", 64 * (hb // 2), 64 * (hb // 2) + 64), True, False)
            todo = [(a, s, x) for x in (0, 1) for a in range(2) for s in sorted(where)]
            for i, (a, s, x) in enumerate(todo):
                qs, lo, d = 8 * a + s, where[s] + a * m, (s ^ k) - s
                l = C("BM", 24 - qs, 152 - qs) if x else C("AD", 160 * d + 16 - qs, 160 * d + 144 - qs)
                mm(o, l, C(IB if x else IA, lo, lo + 2 * m * 63 + 1, 2 * m), False, i == len(todo) - 1)
        emit("v", lambda e: e.transpose(T.T1[:], T.T0[:]), [("T0", 0)], ("T1", 0))
        cp(X("K"), ("T1", T.T1[:].indirect(T.SEL[:, 4 * t:4 * t + 4])), more=[("SEL", 0)])
        ts(X("kz"), X("K"), H, A_.is_lt, float(WC), A_.mult)
        tt(X("ky"), X("kz"), X("K"), A_.add)
        ts(X("LKL"), X("ky"), nH64, A_.add, float(WC + 64), A_.min)
        ts(X("LKR"), X("ky"), nH, A_.add, float(WC), A_.min)
        for side in range(2):
            act(("TL%d" % side, T.TL[:, 512 * side:512 * side + 512]), win("LKL", 32 * side, 32 * side + 32), more=wm("LKL"))
            tt(C("VR", 512 * side, 512 * side + 512), win("LKR", 32 * side, 32 * side + 32), C("XR", xb, xb + 512), (A_.is_gt, A_.is_lt)[side], more=wm("LKR"))
        o = C("PCN", 0, 64)
        for i in range(16):
            mm(o, C("EM", 24 - i, 152 - i), C("VR", i, None, 16), i == 0, False)
        mm(C("PDM", 0, 128), X("ID"), X("ZB"), True, False)
        for par in range(2):
            for side in range(2):
                c = slice(512 * side + par, 512 * side + 512, 2)
                tt(("VL%d" % par, T.VL[:, c]), ("TL%d" % side, T.TL[:, c]), C("PP2", par, 512, 2), (A_.is_lt, A_.is_gt)[side])
        if t == 0:
            p34 = fcol(p3i, 4.0, A_.mult)
            p347 = newf()
            tt(p347, p34, p7, A_.add)
            ts(C("j2", 0, 8), C("j1", 0, 8), 4, A_.bitwise_and)
            ts(C("j3", 0, 8), C("j1", 0, 8), 3, A_.bitwise_and)
            ts(C("j2", 0, 8), C("j2", 0, 8), 16, A_.mult, p347, A_.add)
            ts(C("j3", 0, 8), C("j3", 0, 8), 8, A_.mult)
            tt(C("j2", 0, 8), C("j2", 0, 8), C("j3", 0, 8), A_.add)
            cp(X("DSL"), C("j2", 0, 8))
        for z in (1, 2):
            act(X("m%d" % z), C("PZ%d" % z, 0, 64), RELU, bias=-0.25)
        o = C("PZ1", 64, 128)
        mm(o, X("ID"), C("NO", 64 * t, 64 * t + 64), True, False)
        mm(o, X("ID"), X("m1"), False, False)
        mm(o, X("ID"), X("m2"), False, True)
        act(X("kf"), X("ky"), IDENT, bias=-float(EC))
        act(X("KH"), X("kf"))
        act(X("GX"), o, SIGN)
        tt(X("KL"), X("kf"), X("KH"), A_.subtract)
        o = C("PCN", 0, 64)
        for i in list(range(0, 16, 2)) + list(range(1, 16, 2)):
            mm(o, C("EM", 24 - i, 152 - i), ("VL%d" % (i % 2), T.VL[:, i::16]), False, False)
        mm(o, X("ID"), X("GX"), False, True)
        dm = [(C("PDM", 64 * side + 32 * a, 64 * side + 32 * a + 32), C("QB", 128 * (2 * a + side), 128 * (2 * a + side) + 128), 32 * side)
              for side in range(2) for a in range(2)]
        for oo, l, w in dm:
            mm(oo, l, C("GX", w, w + 32), False, False)
        ts(X("REV"), o, 0.0, A_.is_equal)
        mm(C("PPF", 0, 64), X("LT"), X("REV"), True, True)
        ts(X("FI"), C("PPF", 0, 64), 0.0, A_.is_lt)
        tt(X("FH"), X("FI"), X("KH"), A_.mult)
        tt(X("FL"), X("FI"), X("KL"), A_.mult)
        for j, (oo, l, w) in enumerate(dm):
            mm(oo, l, C("FI", w, w + 32), False, j == 3)
        o = C("PCH", 0, 8)
        for x in ("FH", "FL"):
            for c in range(8):
                mm(o, C("C1", 8 - c, 136 - c), C(x, c, None, 8), x == "FH" and c == 0, x == "FL" and c == 7)
        oc = C("SB0", t * B1 + 128, t * B1 + 192)
        act(X("DP"), C("PDM", 0, 128))
        act(X("DS"), ("DP", T.DP[:].indirect(T.DSL[:])), more=[("DSL", 0)])
        tt(X("o1"), C("DS", 0, 64), C("DS", 64, 128), A_.add)
        tt(X("o2"), X("o1"), oc, A_.mult)
        ts(X("CLS"), o, EH, A_.add, float(WC + 128), A_.min)
        sides = (("PPF", 0), ("PCH", 1))
        for b, side in sides:
            w = 128 * t + 64 * side
            mm(C(b, 64, 128), C("IDF", 0, 128), C("XW", w, w + 64), True, False)
        tt(X("o3"), oc, X("o2"), A_.subtract)
        tt(X("EN"), win("CLS", 0, 8), X("DS"), A_.mult, more=wm("CLS"))
        tt(X("n1"), C("EN", 0, 64), C("EN", 64, 128), A_.add)
        sb = "SB%d" % (t + 1)
        nw = C(sb, 128, 192)
        tt(nw, X("n1"), X("o3"), A_.add)
        ts(X("nz"), nw, H, A_.is_lt, float(WC), A_.mult)
        tt(X("ny"), X("nz"), nw, A_.add)
        ts(X("LN"), X("ny"), nHs, A_.add, capN, A_.min)
        cp(("U2a", T.U2[:, 0:384]), win("LN", 0, 24), more=wm("LN"))
        act(("U2b", T.U2[:, 384:1024]), win("LN", 24, 64), more=wm("LN"))
        act(X("FG"), nw, IDENT, scale=-1.0, bias=float(EC))
        for b, side in sides:
            mm(C(b, 64, 128), C("SL", 128 * side, 128 * side + 128), X("FG"), False, True)
        if t < 2:
            need("g", lastw["U2a"])
            need("g", lastw["U2b"])
            g.remote_dma_fused([RemoteDMATransfer(dst_ids=[dst(topo, h)], dma_engine_mask=1 << topo.engines(core, h)[j],
                                                  remote_sem=T.sem["go%d" % (t + 1)]) for j, h in enumerate(mine)], local_sem=T.sem.ls)
            nls[0] += len(mine)

        def numbers():
            ts(X("y4"), nw, float(WC), A_.is_ge, 4736.0, A_.mult)
            ys = [("yy%d" % j, T.yy[:, 64 * j:64 * j + 64]) for j in range(3)]
            for j, d in enumerate((2880, 576, 192)):
                act(ys[j], nw, IDENT, scale=1.0 / d, bias=-(d - 1) / 2.0 / d)
            for big in (12582912.0, -12582912.0):
                for y in ys:
                    act(y, y, IDENT, bias=big)
            o = C("PG2", 0, 64)
            for j, r in enumerate([nw, X("y4")] + ys):
                w = max(0, j - 1)
                mm(o, C("IDF", 128 * w, 128 * w + 128), r, j == 0, j == 4)
            act(X("YO"), o)
            dma("y", "oO%d" % t, [(T.yo[:, 64 * t:64 * t + 64], T.YO[:])], rd=["YO"])

        if t == 2:
            numbers()
        for hf, lo, hi in (("a", 0, 384), ("b", 384, 1024)):
            emit("v", lambda e, c=slice(lo, hi): e.tensor_tensor_scan(T.SC[:, c], T.RS[:, c], T.U2[:, c], 0.0, A_.add, A_.max),
                 [("RS", 0), ("U2" + hf, 0)], ("SC" + hf, 0))
        for b, side in sides:
            tt(C("ww", 64 * side, 64 * side + 64), C("SC", 7 + 8 * side, None, 16), C(b, 64, 128), A_.max, more=[("SCa", 0), ("SCb", 0)])
        act(C("wn", 0, 64), C("ww", 64, 128), IDENT, scale=-1.0, bias=temp)
        act(C("wn", 64, 128), C("ww", 0, 64), IDENT, scale=-1.0 if t < 2 else 1.0, bias=temp if t < 2 else ntemp)
        tt(X("ws"), C("ww", 0, 64), C("ww", 64, 128), A_.subtract)
        ts(C("wi", 0, 64), X("ws"), 0.5, A_.mult, -0.25, A_.add)
        if t < 2:
            ts(C("wi", 64, 128), X("ws"), -0.5, A_.mult, 0.25, A_.add)
            tt(C(sb, 0, 128), X("wn"), X("wi"), A_.min)
            send(t + 1, sb)
            spread(t + 1, sb)
            act(X("YL"), C(sb, 64, 128), scale=-1.0)
        else:
            tt(C(sb, 0, 64), C("wn", 0, 64), C("wi", 0, 64), A_.min)
            tt(X("YL"), C("wn", 64, 128), C("wi", 0, 64), A_.max)
        dma("y", "oR%d" % t, [(T.yr[:, 64 * t:64 * t + 64], T[sb][:, 0:64])], rd=[sb])
        dma("y", "oL%d" % t, [(T.yl[:, 64 * t:64 * t + 64], T.YL[:])], rd=["YL"])
        if t < 2:
            lists(t + 1)
            sels(t + 1)
            own_walls(t + 1)
            act(X("PP2"), C("XN", 512 * t + 512, 512 * t + 1024))
            empties(t + 1)
            diffs(((2, 3, 5), (6,))[t], ((2,), ())[t])
            numbers()
    g.wait_ge(T.sem.ls, nls[0])
    for sem, c in cnt.items():
        if known["g"].get(sem, 0) < c:
            g.wait_ge(T.sem[sem], c)
